import numpy as np
import ml_dtypes


def mxq(x, axis, fmt="e4m3"):
    dtype, down = {"e4m3": (ml_dtypes.float8_e4m3fn, 7), "e5m2": (ml_dtypes.float8_e5m2, 14)}[fmt]
    v = np.moveaxis(np.asarray(x, np.float32).astype(ml_dtypes.bfloat16).astype(np.float64), axis, -1)
    blocks = v.reshape(v.shape[:-1] + (-1, 32))
    amax = np.abs(blocks).max(-1, keepdims=True)
    byte = np.maximum(np.where(amax > 0, np.frexp(amax)[1] - 1 + 127, 0) - down, 1)
    scale = np.exp2(byte - 127.0)
    codes = (blocks / scale).astype(np.float32).astype(dtype).astype(np.float64)
    return np.moveaxis((codes * scale).reshape(v.shape), -1, axis)


WIDE = False


def mx_kscale(k):
    if not WIDE:
        return np.ones(k)
    levels = np.array([10, -10, 5, -5, 0])
    if k % 512:
        return np.exp2(np.random.permutation(np.resize(levels, k // 32))).repeat(32)
    a = np.empty((k // 512, 16))
    for p in range(k // 512):
        a[p, :8] = np.random.permutation(np.resize(levels, 8))
        for g in range(8):
            far = levels[np.abs(levels - a[p, g]) >= 10]
            a[p, g + 8] = far[np.random.randint(len(far))]
    return np.exp2(a.ravel()).repeat(32)


BF16 = ml_dtypes.bfloat16


def bf(x):
    return np.asarray(x, np.float32).astype(BF16)


def f64(x):
    return np.asarray(x).astype(np.float64)


T, C, E = 1536, 512, 1024


def silu(z):
    return z * (0.5 * (1.0 + np.tanh(0.5 * z)))


def draw0():
    s = mx_kscale(C)
    r = mx_kscale(E)
    t = mx_kscale(T)
    lam = np.random.uniform(-1.0, 1.0, T)
    sigma = np.exp(lam)
    phase = lam[:, None] * (16.0 * np.random.standard_normal(E // 2))[None, :]
    emb = np.sqrt(2.0) * np.concatenate([np.sin(phase), np.cos(phase)], axis=1)
    noisy = np.random.standard_normal((T, C)) + sigma[:, None] * np.random.standard_normal((T, C))
    return {"x": bf(noisy * s),
            "sigma": bf(sigma),
            "emb": bf(emb * r),
            "w": bf(np.random.standard_normal((C, C)) / np.sqrt(C) / s[:, None]),
            "b": bf(0.3 * np.random.standard_normal(C)),
            "v": bf(0.5 * np.random.standard_normal((E, 2 * C)) / np.sqrt(E) / r[:, None]),
            "vb": bf(0.3 * np.random.standard_normal(2 * C)),
            "d": bf((1.0 + 0.1 * np.random.standard_normal(T)) * t),
            "a": bf(np.random.standard_normal((T, T)) / np.sqrt(T) / t),
            "c": bf(0.3 * np.random.standard_normal(T)),
            "k": bf(1.0 + 0.1 * np.random.standard_normal(C))}


def core(x, sigma, emb, w, b, v, vb, d, a, c, k):
    sig = f64(sigma)[:, None]
    h = mxq(f64(x), 1, "e4m3") @ mxq(f64(w), 0, "e4m3")
    h = h / np.sqrt(1.0 + sig * sig) + f64(b)[None, :]
    m = (mxq(f64(emb), 1, "e4m3") @ mxq(f64(v), 0, "e4m3")) + f64(vb)[None, :]
    gamma = m[:, :C]
    beta = m[:, C:]
    y = silu(h * (1.0 + gamma) + beta) * f64(d)[:, None]
    o = mxq(f64(a), 1, "e4m3") @ mxq(y, 0, "e4m3")
    return (o + f64(c)[:, None] + f64(k)[None, :] * h) / sig


def e4m3fn_bytes(y):
    return np.clip(np.asarray(y, np.float64), -448.0, 448.0).astype(np.float32).astype(ml_dtypes.float8_e4m3fn).view(np.uint8)


def e4m3fn_values(b):
    return np.asarray(b, np.uint8).view(ml_dtypes.float8_e4m3fn).astype(np.float64)


def setup_inputs():
    d = draw0()
    x0 = np.asarray(d['a']).astype(np.float64)
    s = (np.max(np.abs(x0), axis=(0,), keepdims=True) / 448.0).astype(np.float32)
    out = {}
    for k, v in d.items():
        if k == 'a':
            out['a_bytes'] = e4m3fn_bytes(x0 / s.astype(np.float64))
            out['a_scale'] = s
        else:
            out[k] = v
    return out


def reference(x, sigma, emb, w, b, v, vb, d, a_bytes, a_scale, c, k):
    return core(x, sigma, emb, w, b, v, vb, d, e4m3fn_values(a_bytes) * a_scale.astype(np.float64), c, k)

@@ -1,0 +1,442 @@
+from contextlib import ExitStack
+
+import concourse.mybir as mybir
+from concourse.masks import make_identity
+
+T, C, E = 1536, 512, 1024
+FLOPS = 2 * (T * C * C + T * E * 2 * C + T * T * C)
+
+F32 = mybir.dt.float32
+BF16 = mybir.dt.bfloat16
+U32 = mybir.dt.uint32
+U8 = mybir.dt.uint8
+F8 = mybir.dt.float8_e4m3fn
+F8X4 = mybir.dt.float8_e4m3fn_x4
+ACT = mybir.ActivationFunctionType
+ADD = mybir.AluOpType.add
+MULT = mybir.AluOpType.mult
+
+P = 128
+J = 4
+KP = P * J
+G = T // KP
+M = C // P
+HC = C // 2
+AV = 0
+ZG = ()
+
+
+def tile_noise_conditioned_score_f4_kernel(tc, x, sigma, emb, w, b, v, vb, d, a_bytes, a_scale, c, k, out):
+    nc = tc.nc
+    with ExitStack() as ctx:
+        pool = ctx.enter_context(tc.tile_pool(name="sb", bufs=1))
+        psum = ctx.enter_context(tc.psum_pool(name="ps", bufs=1))
+
+        def sb(shape, dtype, tag, bufs=1):
+            return pool.tile(shape, dtype, name=tag, tag=tag, bufs=bufs, align_bytes=64)
+
+        def ps(tag, bufs):
+            return psum.tile([P, KP], F32, name=tag, tag=tag, bufs=bufs)
+
+        x_v = x.rearrange("(g p t) n -> g p t n", g=G, p=P)
+        e_v = emb.rearrange("(g p t) n -> g p t n", g=G, p=P)
+        a_v = a_bytes.rearrange("(g p t) n -> g p t n", g=G, p=P)
+        v_v = v.rearrange("(g p j) n -> g p j n", g=2, p=P)
+        x_raw, e_raw, v_raw, a_raw = {}, {}, {}, {}
+
+        def load_x(g):
+            x_raw[g] = sb([P, J, C], BF16, "x_raw", 2)
+            nc.sync.dma_start(out=x_raw[g][:], in_=x_v[g])
+
+        def load_e(g):
+            e_raw[g] = sb([P, J, E], BF16, "e_raw", 2)
+            for h in range(2):
+                nc.sync.dma_start(out=e_raw[g][:, 2 * h : 2 * h + 2, :], in_=e_v[g][:, 2 * h : 2 * h + 2, :])
+
+        def load_a(g, h):
+            a_raw[g, h] = sb([P, 2, T], U8, "a_raw", 4)
+            nc.sync.dma_start(out=a_raw[g, h][:], in_=a_v[g][:, 2 * h : 2 * h + 2, :])
+
+        def load_v(e):
+            v_raw[e] = sb([P, J, 2 * C], BF16, "k8", 3)
+            nc.sync.dma_start(out=v_raw[e][:], in_=v_v[e])
+
+        w_raw = sb([P, J, C], BF16, "w_raw")
+        asc = sb([P, T], F32, "asc")
+        nc.sync.dma_start(out=asc[:], in_=a_scale.rearrange("o k -> (o k)").partition_broadcast(P))
+        load_a(0, 0)
+        nc.sync.dma_start(out=w_raw[:], in_=w.rearrange("(p j) n -> p j n", j=J))
+        load_x(0)
+        load_e(0)
+        load_v(0)
+        load_v(1)
+        load_a(0, 1)
+        load_x(1)
+        load_e(1)
+        load_a(1, 0)
+
+        rows = sb([P, P], BF16, "rows")
+        nc.vector.memset(rows[:], 0.0)
+        tok = {}
+        for nm, vec in (("sigma", sigma), ("d", d), ("c", c)):
+            tok[nm] = sb([P, G, J], BF16, "tok_" + nm)
+            nc.scalar.dma_start(out=tok[nm][:], in_=vec.rearrange("(g p t) -> p g t", g=G, p=P))
+        nc.scalar.dma_start(out=rows[0:4, :], in_=b.rearrange("(m p) -> m p", p=P))
+        nc.scalar.dma_start(out=rows[4:12, :], in_=vb.rearrange("(m p) -> m p", p=P))
+        nc.scalar.dma_start(out=rows[12:16, :], in_=k.rearrange("(m p) -> m p", p=P))
+        ident = sb([P, P], F32, "ident")
+        make_identity(nc, ident[:])
+
+        def vec12(tag):
+            return sb([P, G * J], F32, tag)
+
+        sig, d4, c4, rsig, crs, sq, rt, r12 = [vec12(n) for n in ("sig", "d4", "c4", "rsig", "crs", "sq", "rt", "r12")]
+        cols, g1 = sb([P, 16], F32, "cols"), sb([P, M], F32, "g1")
+        r_t = sb([P, G, KP], F32, "r_t")
+        rows32 = sb([P, P], F32, "rows32")
+        dummy = sb([P, 1], F32, "dummy")
+
+        def flat(nm):
+            return tok[nm][:].rearrange("p g t -> p (g t)")
+
+        def head_vec():
+            nc.vector.tensor_copy(out=sig[:], in_=flat("sigma"))
+            nc.vector.tensor_mul(out=sq[:], in0=sig[:], in1=sig[:])
+            nc.scalar.activation(out=rt[:], in_=sq[:], func=ACT.Sqrt, bias=1.0)
+            nc.scalar.activation(out=dummy[:], in_=rt[:, 0:1], func=ACT.Silu)
+            nc.vector.reciprocal(out=rsig[:], in_=sig[:])
+            nc.vector.reciprocal(out=r12[:], in_=rt[:])
+
+        def head_vec2():
+            nc.vector.tensor_copy(out=d4[:], in_=flat("d"))
+            nc.vector.tensor_copy(out=c4[:], in_=flat("c"))
+            nc.vector.tensor_mul(out=crs[:], in0=c4[:], in1=rsig[:])
+            nc.vector.tensor_copy(out=rows32[:], in_=rows[:])
+            cps = ps("fin", 2)
+            nc.tensor.transpose(cps[:, 0:P], rows32[:], ident[:])
+            nc.vector.tensor_copy(out=cols[:], in_=cps[:, 0:16])
+            nc.vector.tensor_scalar_add(out=g1[:], in0=cols[:, 4:8], scalar1=1.0)
+
+        def spread_r(g):
+            rps = ps("fin", 2)
+            for t in range(J):
+                col = g * J + t
+                nc.tensor.matmul(
+                    rps[:, t * P : (t + 1) * P],
+                    lhsT=r12[:, col : col + 1].to_broadcast([P, P]),
+                    rhs=ident[:],
+                    start=True,
+                    stop=True,
+                )
+            nc.scalar.copy(out=r_t[:, g, :], in_=rps[:])
+
+        def copy_on(engine, out, in_):
+            if engine == "s":
+                nc.scalar.copy(out=out, in_=in_)
+            else:
+                nc.vector.tensor_copy(out=out, in_=in_)
+
+        def quantize(grouped, codes, scales):
+            nc.vector.quantize_mx(out=codes.bitcast(F8X4), scales=scales, in_=grouped.rearrange("p n j -> p (n j)"))
+
+        def turn(row_tiles, k0, grouped, engine):
+            bank = ps("tin", 2)
+            bv = bank[:].rearrange("p (i u r) -> p i u r", i=2, u=2)
+            for i, rt_ in enumerate(row_tiles):
+                words = rt_.bitcast(F32)
+                for u in range(2):
+                    nc.tensor.transpose(bv[:, i, u, :], words[:, k0 // 2 + u : (k0 + KP) // 2 : 2], ident[:])
+            gw = grouped.rearrange("p n j -> p (n j)").bitcast(F32).rearrange("p (i r u) -> p i u r", i=2, u=2)
+            copy_on(engine, gw.rearrange("p i u r -> p i r u"), bv.rearrange("p i u r -> p i r u"))
+
+        w_c, w_s = sb([P, C], U32, "w_c"), sb([P, C], U8, "w_s")
+        v_c, v_s = sb([P, 2, 2 * C], U32, "v_c"), sb([P, 2, 2 * C], U8, "v_s")
+        x_c, x_s = sb([P, G, KP], U32, "x_c"), sb([P, G, KP], U8, "x_s")
+        e_c, e_s = sb([P, G, 2, KP], U32, "e_c"), sb([P, G, 2, KP], U8, "e_s")
+        a_c, a_s = sb([P, G, G, KP], U32, "a_c"), sb([P, G, G, KP], U8, "a_s")
+        y_c, y_s = sb([P, G, C], U32, "y_c"), sb([P, G, C], U8, "y_s")
+
+        wgs = {}
+
+        def w_copy(n, engine):
+            wgs["w", n] = sb([P, HC, J], BF16, "wg", 3)
+            copy_on(engine, wgs["w", n][:], w_raw[:, :, n : n + HC].rearrange("p j n -> p n j"))
+
+        def w_quant(n):
+            quantize(wgs["w", n][:], w_c[:, n : n + HC], w_s[:, n : n + HC])
+
+        def v_copy(e, n, engine):
+            wgs[e, n] = sb([P, HC, J], BF16, "wg", 3)
+            copy_on(engine, wgs[e, n][:], v_raw[e][:, :, n : n + HC].rearrange("p j n -> p n j"))
+
+        def v_quant(e, n):
+            quantize(wgs[e, n][:], v_c[:, e, n : n + HC], v_s[:, e, n : n + HC])
+
+        xgs = {}
+
+        def x_turn(g, h, engine):
+            if h == 0:
+                xgs["x", g] = sb([P, KP, J], BF16, "xg", 3)
+            turn([x_raw[g][:, 2 * h + i, :] for i in range(2)], 0, xgs["x", g][:, 2 * h * P : 2 * (h + 1) * P, :], engine)
+
+        def x_quant(g):
+            quantize(xgs["x", g][:], x_c[:, g, :], x_s[:, g, :])
+
+        def e_turn(g, e, h, engine):
+            if h == 0:
+                xgs[e, g] = sb([P, KP, J], BF16, "xg", 3)
+            turn([e_raw[g][:, 2 * h + i, :] for i in range(2)], e * KP, xgs[e, g][:, 2 * h * P : 2 * (h + 1) * P, :], engine)
+
+        def e_quant(g, e):
+            quantize(xgs[e, g][:], e_c[:, g, e, :], e_s[:, g, e, :])
+
+        prods, ags = {}, {}
+
+        def product(g, t):
+            pr = sb([P, T], BF16, "prod", 6)
+            nc.vector.tensor_tensor(out=pr[:], in0=a_raw[g, t // 2][:, t % 2, :].bitcast(F8), in1=asc[:], op=MULT)
+            prods[g, t] = pr
+
+        def a_turn(g, h, q, engine):
+            if h == 0:
+                ags[g, q] = sb([P, KP, J], BF16, "ag", 5)
+            turn([prods[g, 2 * h + i][:] for i in range(2)], q * KP, ags[g, q][:, 2 * h * P : 2 * (h + 1) * P, :], engine)
+
+        def a_quant(g, q):
+            quantize(ags[g, q][:], a_c[:, g, q, :], a_s[:, g, q, :])
+
+        def mm(bank, pairs):
+            for i, (l, ls, r, rs) in enumerate(pairs):
+                nc.tensor.matmul_mx(
+                    out=bank, lhsT=l.bitcast(F8X4), lhsT_scale=ls, rhs=r.bitcast(F8X4), rhs_scale=rs,
+                    start=(i == 0), stop=(i == len(pairs) - 1),
+                )
+
+        units = [(g, m) for hf in range(2) for g in range(G) for m in (2 * hf, 2 * hf + 1)]
+        st = {}
+
+        def u_mx(n):
+            g, m = units[n]
+            cs = slice(m * P, (m + 1) * P)
+            bs = slice(C + m * P, C + (m + 1) * P)
+            st["p", n], st["g", n], st["b", n] = ps("acc", 4), ps("acc", 4), ps("acc", 4)
+            mm(st["p", n][:], [(w_c[:, cs], w_s[:, cs], x_c[:, g, :], x_s[:, g, :])])
+            for nm, s_ in (("g", cs), ("b", bs)):
+                mm(st[nm, n][:], [(v_c[:, e, s_], v_s[:, e, s_], e_c[:, g, e, :], e_s[:, g, e, :]) for e in range(2)])
+
+        def u_hp(n):
+            g, m = units[n]
+            st["hp", n] = sb([P, KP], F32, "hp", 2)
+            nc.vector.tensor_mul(out=st["hp", n][:], in0=st["p", n][:], in1=r_t[:, g, :])
+
+        def u_h(n):
+            g, m = units[n]
+            st["h", n] = sb([P, KP], F32, "h", 2)
+            nc.scalar.activation(out=st["h", n][:], in_=st["hp", n][:], func=ACT.Identity, bias=cols[:, m : m + 1])
+            if m % 2 == 0:
+                st["kh", g, m // 2] = sb([P, 2, KP], F32, "kh", 2)
+            nc.gpsimd.tensor_scalar(
+                out=st["kh", g, m // 2][:, m % 2, :], in0=st["hp", n][:],
+                scalar1=cols[:, m : m + 1], scalar2=cols[:, 12 + m : 13 + m], op0=ADD, op1=MULT,
+            )
+
+        def u_z0(n):
+            g, m = units[n]
+            st["z0", n] = sb([P, KP], F32, "z0", 2)
+            nc.vector.scalar_tensor_tensor(
+                out=st["z0", n][:], in0=st["g", n][:], scalar=g1[:, m : m + 1], in1=st["h", n][:], op0=ADD, op1=MULT
+            )
+
+        def u_z(n):
+            g, m = units[n]
+            st["z", n] = sb([P, KP], F32, "z", 2)
+            if n in ZG:
+                bt = sb([P, KP], F32, "bt", 2)
+                nc.scalar.activation(out=bt[:], in_=st["b", n][:], func=ACT.Identity, bias=cols[:, 8 + m : 9 + m])
+                nc.gpsimd.tensor_tensor(out=st["z", n][:], in0=bt[:], in1=st["z0", n][:], op=ADD)
+                return
+            nc.vector.scalar_tensor_tensor(
+                out=st["z", n][:], in0=st["b", n][:], scalar=cols[:, 8 + m : 9 + m], in1=st["z0", n][:], op0=ADD, op1=ADD
+            )
+
+        def u_t1(n):
+            st["y", n] = ps("fin", 2)
+            for t in range(J):
+                ts_ = slice(t * P, (t + 1) * P)
+                nc.tensor.transpose(st["y", n][:, ts_], st["z", n][:, ts_], ident[:])
+
+        def u_silu(n):
+            st["s", n] = sb([P, KP], F32, "s", 2)
+            nc.scalar.activation(out=st["s", n][:], in_=st["y", n][:], func=ACT.Silu)
+
+        def u_y(n):
+            g, m = units[n]
+            if m % 2 == 0:
+                st["yg", g, m // 2] = sb([P, HC, J], BF16, "yg", 2)
+            i = m % 2
+            nc.gpsimd.tensor_tensor(
+                out=st["yg", g, m // 2][:, i * P : (i + 1) * P, :],
+                in0=st["s", n][:].rearrange("p (t c) -> p c t", t=J),
+                in1=d4[:, g * J : (g + 1) * J].unsqueeze(1).to_broadcast([P, P, J]),
+                op=MULT,
+            )
+
+        def y_quant(g, hf):
+            cs = slice(hf * HC, (hf + 1) * HC)
+            quantize(st["yg", g, hf][:], y_c[:, g, cs], y_s[:, g, cs])
+
+        u_t = {}
+
+        def skip(g, hf, tp):
+            kh = st["kh", g, hf]
+            bank = ps("fin", 2)
+            for i in range(2):
+                for m in range(2):
+                    t = 2 * tp + i
+                    nc.tensor.transpose(bank[:, (2 * i + m) * P : (2 * i + m + 1) * P], kh[:, m, t * P : (t + 1) * P], ident[:])
+            if g not in u_t:
+                u_t[g] = sb([P, J, C], F32, "k8", 3)
+            for i in range(2):
+                col = g * J + 2 * tp + i
+                nc.scalar.activation(
+                    out=u_t[g][:, 2 * tp + i, hf * HC : (hf + 1) * HC], in_=bank[:, i * HC : (i + 1) * HC],
+                    func=ACT.Identity, scale=rsig[:, col : col + 1], bias=crs[:, col : col + 1],
+                )
+
+        o_v = out.rearrange("(g p t) n -> g p t n", g=G, p=P)
+
+        def o_mx(g, hf, tp):
+            bank = ps("acc", 4)
+            st["o", g, hf, tp] = bank
+            cs = slice(hf * HC, (hf + 1) * HC)
+            for i in range(2):
+                ts_ = slice((2 * tp + i) * P, (2 * tp + i + 1) * P)
+                mm(bank[:, i * HC : (i + 1) * HC], [(a_c[:, g, q, ts_], a_s[:, g, q, ts_], y_c[:, q, cs], y_s[:, q, cs]) for q in range(G)])
+
+        def o_fin(g, hf, tp):
+            bank = st["o", g, hf, tp]
+            cs = slice(hf * HC, (hf + 1) * HC)
+            for i in range(2):
+                t = 2 * tp + i
+                col = g * J + t
+                nc.vector.scalar_tensor_tensor(
+                    out=u_t[g][:, t, cs], in0=bank[:, i * HC : (i + 1) * HC], scalar=rsig[:, col : col + 1],
+                    in1=u_t[g][:, t, cs], op0=MULT, op1=ADD,
+                )
+
+        def o_store(g, hf, tp, n):
+            cs = slice(hf * HC, (hf + 1) * HC)
+            nc.sync.dma_start(out=o_v[g][:, 2 * tp : 2 * tp + 2 * n, cs], in_=u_t[g][:, 2 * tp : 2 * tp + 2 * n, cs])
+
+        head_vec()
+        w_copy(0, "v")
+        w_quant(0)
+        head_vec2()
+        for h in range(2):
+            x_turn(0, h, "s")
+        x_quant(0)
+        spread_r(0)
+        for e in range(2):
+            for h in range(2):
+                e_turn(0, e, h, "s")
+        product(0, 0)
+        e_quant(0, 0)
+        e_quant(0, 1)
+        v_copy(0, 0, "s")
+        v_copy(0, C, "s")
+        product(0, 1)
+        v_quant(0, 0)
+        v_quant(0, C)
+        v_copy(1, 0, "v")
+        v_copy(1, C, "s")
+        v_quant(1, 0)
+        v_quant(1, C)
+        spread_r(1)
+        spread_r(2)
+        load_a(1, 1)
+        load_x(2)
+        load_e(2)
+        load_a(2, 0)
+        load_a(2, 1)
+
+        N = len(units)
+        late_w = [("v", 0, HC), ("v", 0, C + HC), ("v", 1, HC), ("v", 1, C + HC), ("w", 0, HC)]
+        a_jobs = [(g, h, q) for g in range(G) for h in range(2) for q in range(G)]
+        a_next = 0
+        p_next = 2
+        for n in range(N + 1):
+            if n < N:
+                u_mx(n)
+                u_hp(n)
+                u_h(n)
+            if n > 0:
+                u_t1(n - 1)
+                u_silu(n - 1)
+                u_y(n - 1)
+            if 2 <= n and n % 2 == 0:
+                g, m = units[n - 2]
+                for tp in range(2):
+                    skip(g, m // 2, tp)
+            if n < len(late_w):
+                nm, e, c0 = late_w[n]
+                if nm == "v":
+                    v_copy(e, c0, "s")
+                else:
+                    w_copy(c0, "s")
+            if n < 4:
+                g = 1 + n // 2
+                if n % 2 == 0:
+                    x_turn(g, 0, "s")
+                    x_turn(g, 1, "s")
+                    e_turn(g, 0, 0, "s")
+                else:
+                    e_turn(g, 0, 1, "s")
+                    e_turn(g, 1, 0, "s")
+                    e_turn(g, 1, 1, "s")
+            if p_next < 12 and n < N:
+                product(p_next // 4, p_next % 4)
+                p_next += 1
+            if n < 4:
+                g = 1 + n // 2
+                if n % 2 == 0:
+                    x_quant(g)
+                else:
+                    e_quant(g, 0)
+                    e_quant(g, 1)
+            if n < N:
+                u_z0(n)
+                u_z(n)
+            na = 1 if n < 4 else 2
+            for i in range(na):
+                if a_next < len(a_jobs):
+                    g, h, q = a_jobs[a_next]
+                    a_turn(g, h, q, "v" if n < AV else "s")
+                    a_next += 1
+                    if h == 1:
+                        a_quant(g, q)
+            if n < len(late_w):
+                nm, e, c0 = late_w[n]
+                if nm == "v":
+                    v_quant(e, c0)
+                else:
+                    w_quant(c0)
+            if n >= 2 and n % 2 == 0:
+                g, m = units[n - 2]
+                y_quant(g, m // 2)
+            if n == 8 or n == 9 or n == 10 or n == 11:
+                pass
+        while a_next < len(a_jobs):
+            g, h, q = a_jobs[a_next]
+            a_turn(g, h, q, "s")
+            a_next += 1
+            if h == 1:
+                a_quant(g, q)
+        for hf in range(2):
+            for g in range(G):
+                for tp in range(2):
+                    o_mx(g, hf, tp)
+                    o_fin(g, hf, tp)
+                    if hf:
+                        o_store(g, hf, tp, 1)
+                if not hf:
+                    o_store(g, hf, 0, 2)

@@ -22,8 +22,355 @@ KP = P * J
 G = T // KP
 M = C // P
 HC = C // 2
-AV = 0
-ZG = ()
+ZV = ()
+VS = ((0, 1, 1),)
+ORDER = [
+    ("d", "x", 0),
+    ("d", "e", 0, 0),
+    ("d", "w"),
+    ("d", "v", 0),
+    ("d", "e", 0, 1),
+    ("d", "v", 1),
+    ("d", "a", 0, 0),
+    ("d", "e", 1, 0),
+    ("d", "x", 1),
+    ("d", "e", 1, 1),
+    ("sq",),
+    ("sp", 1),
+    ("wcp", 0),
+    ("turn", "x", 0, 0, 1),
+    ("turn", "e", 0, 0, 0),
+    ("wq", 0),
+    ("turn", "x", 0, 0, 0),
+    ("d", "x", 2),
+    ("d", "a", 0, 1),
+    ("spc", 1),
+    ("turn", "e", 0, 1, 0),
+    ("sp", 0),
+    ("cols1",),
+    ("cp", "e", 0, 0, 0),
+    ("vcp", 0, 0, 1),
+    ("turn", "e", 0, 0, 1),
+    ("vcp", 0, 0, 0),
+    ("vq", 0, 0, 1),
+    ("cp", "x", 0, 0, 1),
+    ("cp", "x", 0, 0, 0),
+    ("wcp", 1),
+    ("vq", 0, 0, 0),
+    ("sqrt",),
+    ("turn", "e", 0, 1, 1),
+    ("d", "e", 2, 0),
+    ("d", "e", 2, 1),
+    ("d", "a", 1, 0),
+    ("d", "a", 1, 1),
+    ("cp", "e", 0, 1, 0),
+    ("spc", 0),
+    ("cp", "e", 0, 0, 1),
+    ("xq", 0),
+    ("sp", 2),
+    ("cp", "e", 0, 1, 1),
+    ("rec",),
+    ("colsT",),
+    ("wq", 1),
+    ("vcp", 0, 1, 1),
+    ("hmx", 0, 0),
+    ("vcp", 0, 1, 0),
+    ("vq", 0, 1, 0),
+    ("spc", 2),
+    ("hr", 0, 0, 1),
+    ("eq", 0, 1),
+    ("hr", 0, 0, 0),
+    ("eq", 0, 0),
+    ("silud",),
+    ("cols2",),
+    ("vq", 0, 1, 1),
+    ("prod", 0, 0),
+    ("turn", "x", 1, 0, 0),
+    ("turn", "x", 1, 0, 1),
+    ("t3", 0),
+    ("cp", "x", 1, 0, 0),
+    ("bmx", 0),
+    ("gmx", 0),
+    ("turn", "e", 1, 0, 0),
+    ("cp", "x", 1, 0, 1),
+    ("turn", "e", 1, 0, 1),
+    ("prod", 0, 1),
+    ("d", "a", 2, 0),
+    ("h", 0),
+    ("cp", "e", 1, 0, 0),
+    ("turn", "e", 1, 1, 0),
+    ("xq", 1),
+    ("cp", "e", 1, 0, 1),
+    ("turn", "e", 1, 1, 1),
+    ("t3", 1),
+    ("hmx", 1, 0),
+    ("bt", 0),
+    ("z0", 0),
+    ("bmx", 1),
+    ("kh", 0),
+    ("gmx", 1),
+    ("cp", "e", 1, 1, 0),
+    ("turn", "x", 2, 0, 0),
+    ("vcp", 1, 0, 0),
+    ("eq", 1, 0),
+    ("vq", 1, 0, 0),
+    ("cp", "e", 1, 1, 1),
+    ("hr", 1, 0, 0),
+    ("hr", 1, 0, 1),
+    ("turn", "x", 2, 0, 1),
+    ("prod", 0, 2),
+    ("h", 1),
+    ("t1", 0),
+    ("cp", "x", 2, 0, 0),
+    ("turn", "e", 2, 0, 0),
+    ("eq", 1, 1),
+    ("cp", "x", 2, 0, 1),
+    ("turn", "e", 2, 0, 1),
+    ("t3", 2),
+    ("vcp", 1, 0, 1),
+    ("bt", 1),
+    ("z0", 1),
+    ("bmx", 2),
+    ("vq", 1, 0, 1),
+    ("kh", 1),
+    ("gmx", 2),
+    ("t2", 0, 0, 0),
+    ("cp", "e", 2, 0, 0),
+    ("turn", "e", 2, 1, 0),
+    ("t2", 0, 0, 1),
+    ("xq", 2),
+    ("silu", 0),
+    ("cp", "e", 2, 0, 1),
+    ("h", 2),
+    ("prod", 0, 3),
+    ("d", "a", 2, 1),
+    ("turn", "e", 2, 1, 1),
+    ("u", 0, 0, 0),
+    ("t1", 1),
+    ("cp", "e", 2, 1, 0),
+    ("u", 0, 0, 1),
+    ("vcp", 1, 1, 0),
+    ("vq", 1, 1, 0),
+    ("eq", 2, 0),
+    ("cp", "e", 2, 1, 1),
+    ("t3", 3),
+    ("hmx", 2, 0),
+    ("bt", 2),
+    ("z0", 2),
+    ("turn", "a", 0, 0, 0),
+    ("bmx", 3),
+    ("kh", 2),
+    ("gmx", 3),
+    ("eq", 2, 1),
+    ("silu", 1),
+    ("hr", 2, 0, 0),
+    ("hr", 2, 0, 1),
+    ("y", 0),
+    ("h", 3),
+    ("prod", 1, 0),
+    ("vcp", 1, 1, 1),
+    ("cp", "a", 0, 0, 0),
+    ("t1", 2),
+    ("vq", 1, 1, 1),
+    ("turn", "a", 0, 1, 0),
+    ("t3", 4),
+    ("bt", 3),
+    ("z0", 3),
+    ("bmx", 4),
+    ("cp", "a", 0, 1, 0),
+    ("kh", 3),
+    ("gmx", 4),
+    ("t2", 1, 0, 0),
+    ("turn", "a", 0, 2, 0),
+    ("t2", 1, 0, 1),
+    ("silu", 2),
+    ("y", 1),
+    ("h", 4),
+    ("prod", 1, 1),
+    ("u", 1, 0, 0),
+    ("t1", 3),
+    ("cp", "a", 0, 2, 0),
+    ("turn", "a", 0, 0, 1),
+    ("u", 1, 0, 1),
+    ("t3", 5),
+    ("hmx", 0, 1),
+    ("bt", 4),
+    ("z0", 4),
+    ("bmx", 5),
+    ("kh", 4),
+    ("gmx", 5),
+    ("cp", "a", 0, 0, 1),
+    ("turn", "a", 0, 1, 1),
+    ("silu", 3),
+    ("hr", 0, 1, 0),
+    ("hr", 0, 1, 1),
+    ("y", 2),
+    ("h", 5),
+    ("prod", 1, 2),
+    ("t1", 4),
+    ("cp", "a", 0, 1, 1),
+    ("turn", "a", 0, 2, 1),
+    ("t3", 6),
+    ("bt", 5),
+    ("z0", 5),
+    ("bmx", 6),
+    ("kh", 5),
+    ("gmx", 6),
+    ("t2", 2, 0, 0),
+    ("cp", "a", 0, 2, 1),
+    ("t2", 2, 0, 1),
+    ("turn", "a", 1, 0, 0),
+    ("silu", 4),
+    ("y", 3),
+    ("h", 6),
+    ("aq", 0, 0),
+    ("u", 2, 0, 0),
+    ("prod", 1, 3),
+    ("t1", 5),
+    ("u", 2, 0, 1),
+    ("cp", "a", 1, 0, 0),
+    ("turn", "a", 1, 1, 0),
+    ("yq", 0, 0),
+    ("t3", 7),
+    ("hmx", 1, 1),
+    ("bt", 6),
+    ("z0", 6),
+    ("aq", 0, 1),
+    ("bmx", 7),
+    ("kh", 6),
+    ("gmx", 7),
+    ("cp", "a", 1, 1, 0),
+    ("turn", "a", 1, 2, 0),
+    ("silu", 5),
+    ("hr", 1, 1, 0),
+    ("hr", 1, 1, 1),
+    ("y", 4),
+    ("h", 7),
+    ("t1", 6),
+    ("prod", 2, 0),
+    ("aq", 0, 2),
+    ("cp", "a", 1, 2, 0),
+    ("turn", "a", 1, 0, 1),
+    ("t3", 8),
+    ("bt", 7),
+    ("z0", 7),
+    ("bmx", 8),
+    ("kh", 7),
+    ("gmx", 8),
+    ("t2", 0, 1, 0),
+    ("t2", 0, 1, 1),
+    ("cp", "a", 1, 0, 1),
+    ("turn", "a", 1, 1, 1),
+    ("silu", 6),
+    ("y", 5),
+    ("h", 8),
+    ("u", 0, 1, 0),
+    ("t1", 7),
+    ("prod", 2, 1),
+    ("u", 0, 1, 1),
+    ("cp", "a", 1, 1, 1),
+    ("turn", "a", 1, 2, 1),
+    ("yq", 1, 0),
+    ("t3", 9),
+    ("hmx", 2, 1),
+    ("bt", 8),
+    ("z0", 8),
+    ("bmx", 9),
+    ("kh", 8),
+    ("gmx", 9),
+    ("cp", "a", 1, 2, 1),
+    ("silu", 7),
+    ("hr", 2, 1, 0),
+    ("hr", 2, 1, 1),
+    ("y", 6),
+    ("turn", "a", 2, 0, 0),
+    ("h", 9),
+    ("t1", 8),
+    ("prod", 2, 2),
+    ("aq", 1, 0),
+    ("cp", "a", 2, 0, 0),
+    ("turn", "a", 2, 1, 0),
+    ("t3", 10),
+    ("bt", 9),
+    ("z0", 9),
+    ("bmx", 10),
+    ("kh", 9),
+    ("gmx", 10),
+    ("t2", 1, 1, 0),
+    ("aq", 1, 1),
+    ("t2", 1, 1, 1),
+    ("silu", 8),
+    ("y", 7),
+    ("cp", "a", 2, 1, 0),
+    ("h", 10),
+    ("turn", "a", 2, 2, 0),
+    ("u", 1, 1, 0),
+    ("t1", 9),
+    ("prod", 2, 3),
+    ("u", 1, 1, 1),
+    ("aq", 1, 2),
+    ("yq", 2, 0),
+    ("t3", 11),
+    ("cp", "a", 2, 2, 0),
+    ("turn", "a", 2, 0, 1),
+    ("bt", 10),
+    ("z0", 10),
+    ("bmx", 11),
+    ("kh", 10),
+    ("gmx", 11),
+    ("silu", 9),
+    ("y", 8),
+    ("h", 11),
+    ("cp", "a", 2, 0, 1),
+    ("turn", "a", 2, 1, 1),
+    ("t1", 10),
+    ("cp", "a", 2, 1, 1),
+    ("bt", 11),
+    ("z0", 11),
+    ("turn", "a", 2, 2, 1),
+    ("kh", 11),
+    ("t2", 2, 1, 0),
+    ("t2", 2, 1, 1),
+    ("silu", 10),
+    ("y", 9),
+    ("cp", "a", 2, 2, 1),
+    ("u", 2, 1, 0),
+    ("t1", 11),
+    ("u", 2, 1, 1),
+    ("aq", 2, 0),
+    ("yq", 0, 1),
+    ("aq", 2, 1),
+    ("silu", 11),
+    ("y", 10),
+    ("aq", 2, 2),
+    ("omx", 0, 0, 0),
+    ("y", 11),
+    ("ofin", 0, 0, 0),
+    ("yq", 1, 1),
+    ("omx", 0, 0, 1),
+    ("ofin", 0, 0, 1),
+    ("omx", 1, 0, 0),
+    ("yq", 2, 1),
+    ("ofin", 1, 0, 0),
+    ("omx", 1, 0, 1),
+    ("ofin", 1, 0, 1),
+    ("omx", 2, 0, 0),
+    ("ofin", 2, 0, 0),
+    ("omx", 2, 0, 1),
+    ("ofin", 2, 0, 1),
+    ("omx", 0, 1, 0),
+    ("ofin", 0, 1, 0),
+    ("omx", 0, 1, 1),
+    ("ofin", 0, 1, 1),
+    ("omx", 1, 1, 0),
+    ("ofin", 1, 1, 0),
+    ("omx", 1, 1, 1),
+    ("ofin", 1, 1, 1),
+    ("omx", 2, 1, 0),
+    ("ofin", 2, 1, 0),
+    ("omx", 2, 1, 1),
+    ("ofin", 2, 1, 1),
+]
 
 
 def tile_noise_conditioned_score_f4_kernel(tc, x, sigma, emb, w, b, v, vb, d, a_bytes, a_scale, c, k, out):
@@ -31,59 +378,36 @@ def tile_noise_conditioned_score_f4_kernel(tc, x, sigma, emb, w, b, v, vb, d, a_
     with ExitStack() as ctx:
         pool = ctx.enter_context(tc.tile_pool(name="sb", bufs=1))
         psum = ctx.enter_context(tc.psum_pool(name="ps", bufs=1))
+        ctx.enter_context(tc.manual_schedule())
 
         def sb(shape, dtype, tag, bufs=1):
             return pool.tile(shape, dtype, name=tag, tag=tag, bufs=bufs, align_bytes=64)
 
-        def ps(tag, bufs):
-            return psum.tile([P, KP], F32, name=tag, tag=tag, bufs=bufs)
+        def ps(tag):
+            return psum.tile([P, KP], F32, name=tag, tag=tag, bufs=4)
 
         x_v = x.rearrange("(g p t) n -> g p t n", g=G, p=P)
         e_v = emb.rearrange("(g p t) n -> g p t n", g=G, p=P)
         a_v = a_bytes.rearrange("(g p t) n -> g p t n", g=G, p=P)
         v_v = v.rearrange("(g p j) n -> g p j n", g=2, p=P)
-        x_raw, e_raw, v_raw, a_raw = {}, {}, {}, {}
+        o_v = out.rearrange("(g p t) n -> g p t n", g=G, p=P)
+        st = {}
 
-        def load_x(g):
-            x_raw[g] = sb([P, J, C], BF16, "x_raw", 2)
-            nc.sync.dma_start(out=x_raw[g][:], in_=x_v[g])
-
-        def load_e(g):
-            e_raw[g] = sb([P, J, E], BF16, "e_raw", 2)
-            for h in range(2):
-                nc.sync.dma_start(out=e_raw[g][:, 2 * h : 2 * h + 2, :], in_=e_v[g][:, 2 * h : 2 * h + 2, :])
-
-        def load_a(g, h):
-            a_raw[g, h] = sb([P, 2, T], U8, "a_raw", 4)
-            nc.sync.dma_start(out=a_raw[g, h][:], in_=a_v[g][:, 2 * h : 2 * h + 2, :])
-
-        def load_v(e):
-            v_raw[e] = sb([P, J, 2 * C], BF16, "k8", 3)
-            nc.sync.dma_start(out=v_raw[e][:], in_=v_v[e])
-
-        w_raw = sb([P, J, C], BF16, "w_raw")
-        asc = sb([P, T], F32, "asc")
-        nc.sync.dma_start(out=asc[:], in_=a_scale.rearrange("o k -> (o k)").partition_broadcast(P))
-        load_a(0, 0)
-        nc.sync.dma_start(out=w_raw[:], in_=w.rearrange("(p j) n -> p j n", j=J))
-        load_x(0)
-        load_e(0)
-        load_v(0)
-        load_v(1)
-        load_a(0, 1)
-        load_x(1)
-        load_e(1)
-        load_a(1, 0)
-
-        rows = sb([P, P], BF16, "rows")
-        nc.vector.memset(rows[:], 0.0)
         tok = {}
+        asv = sb([P, G * J], F32, "asv")
         for nm, vec in (("sigma", sigma), ("d", d), ("c", c)):
             tok[nm] = sb([P, G, J], BF16, "tok_" + nm)
-            nc.scalar.dma_start(out=tok[nm][:], in_=vec.rearrange("(g p t) -> p g t", g=G, p=P))
+        nc.scalar.dma_start(out=tok["sigma"][:], in_=sigma.rearrange("(g p t) -> p g t", g=G, p=P))
+        nc.scalar.dma_start(
+            out=asv[:].rearrange("p (g t) -> p g t", g=G), in_=a_scale.rearrange("o (g p t) -> p (o g) t", g=G, p=P)
+        )
+        rows = sb([P, P], BF16, "rows")
+        nc.vector.memset(rows[:], 0.0)
         nc.scalar.dma_start(out=rows[0:4, :], in_=b.rearrange("(m p) -> m p", p=P))
         nc.scalar.dma_start(out=rows[4:12, :], in_=vb.rearrange("(m p) -> m p", p=P))
         nc.scalar.dma_start(out=rows[12:16, :], in_=k.rearrange("(m p) -> m p", p=P))
+        nc.scalar.dma_start(out=tok["d"][:], in_=d.rearrange("(g p t) -> p g t", g=G, p=P))
+        nc.scalar.dma_start(out=tok["c"][:], in_=c.rearrange("(g p t) -> p g t", g=G, p=P))
         ident = sb([P, P], F32, "ident")
         make_identity(nc, ident[:])
 
@@ -92,63 +416,10 @@ def tile_noise_conditioned_score_f4_kernel(tc, x, sigma, emb, w, b, v, vb, d, a_
 
         sig, d4, c4, rsig, crs, sq, rt, r12 = [vec12(n) for n in ("sig", "d4", "c4", "rsig", "crs", "sq", "rt", "r12")]
         cols, g1 = sb([P, 16], F32, "cols"), sb([P, M], F32, "g1")
-        r_t = sb([P, G, KP], F32, "r_t")
         rows32 = sb([P, P], F32, "rows32")
         dummy = sb([P, 1], F32, "dummy")
-
-        def flat(nm):
-            return tok[nm][:].rearrange("p g t -> p (g t)")
-
-        def head_vec():
-            nc.vector.tensor_copy(out=sig[:], in_=flat("sigma"))
-            nc.vector.tensor_mul(out=sq[:], in0=sig[:], in1=sig[:])
-            nc.scalar.activation(out=rt[:], in_=sq[:], func=ACT.Sqrt, bias=1.0)
-            nc.scalar.activation(out=dummy[:], in_=rt[:, 0:1], func=ACT.Silu)
-            nc.vector.reciprocal(out=rsig[:], in_=sig[:])
-            nc.vector.reciprocal(out=r12[:], in_=rt[:])
-
-        def head_vec2():
-            nc.vector.tensor_copy(out=d4[:], in_=flat("d"))
-            nc.vector.tensor_copy(out=c4[:], in_=flat("c"))
-            nc.vector.tensor_mul(out=crs[:], in0=c4[:], in1=rsig[:])
-            nc.vector.tensor_copy(out=rows32[:], in_=rows[:])
-            cps = ps("fin", 2)
-            nc.tensor.transpose(cps[:, 0:P], rows32[:], ident[:])
-            nc.vector.tensor_copy(out=cols[:], in_=cps[:, 0:16])
-            nc.vector.tensor_scalar_add(out=g1[:], in0=cols[:, 4:8], scalar1=1.0)
-
-        def spread_r(g):
-            rps = ps("fin", 2)
-            for t in range(J):
-                col = g * J + t
-                nc.tensor.matmul(
-                    rps[:, t * P : (t + 1) * P],
-                    lhsT=r12[:, col : col + 1].to_broadcast([P, P]),
-                    rhs=ident[:],
-                    start=True,
-                    stop=True,
-                )
-            nc.scalar.copy(out=r_t[:, g, :], in_=rps[:])
-
-        def copy_on(engine, out, in_):
-            if engine == "s":
-                nc.scalar.copy(out=out, in_=in_)
-            else:
-                nc.vector.tensor_copy(out=out, in_=in_)
-
-        def quantize(grouped, codes, scales):
-            nc.vector.quantize_mx(out=codes.bitcast(F8X4), scales=scales, in_=grouped.rearrange("p n j -> p (n j)"))
-
-        def turn(row_tiles, k0, grouped, engine):
-            bank = ps("tin", 2)
-            bv = bank[:].rearrange("p (i u r) -> p i u r", i=2, u=2)
-            for i, rt_ in enumerate(row_tiles):
-                words = rt_.bitcast(F32)
-                for u in range(2):
-                    nc.tensor.transpose(bv[:, i, u, :], words[:, k0 // 2 + u : (k0 + KP) // 2 : 2], ident[:])
-            gw = grouped.rearrange("p n j -> p (n j)").bitcast(F32).rearrange("p (i r u) -> p i u r", i=2, u=2)
-            copy_on(engine, gw.rearrange("p i u r -> p i r u"), bv.rearrange("p i u r -> p i r u"))
-
+        asc = sb([P, T], F32, "asc")
+        w_raw = sb([P, J, C], BF16, "w_raw")
         w_c, w_s = sb([P, C], U32, "w_c"), sb([P, C], U8, "w_s")
         v_c, v_s = sb([P, 2, 2 * C], U32, "v_c"), sb([P, 2, 2 * C], U8, "v_s")
         x_c, x_s = sb([P, G, KP], U32, "x_c"), sb([P, G, KP], U8, "x_s")
@@ -156,54 +427,17 @@ def tile_noise_conditioned_score_f4_kernel(tc, x, sigma, emb, w, b, v, vb, d, a_
         a_c, a_s = sb([P, G, G, KP], U32, "a_c"), sb([P, G, G, KP], U8, "a_s")
         y_c, y_s = sb([P, G, C], U32, "y_c"), sb([P, G, C], U8, "y_s")
 
-        wgs = {}
+        def flat(nm):
+            return tok[nm][:].rearrange("p g t -> p (g t)")
 
-        def w_copy(n, engine):
-            wgs["w", n] = sb([P, HC, J], BF16, "wg", 3)
-            copy_on(engine, wgs["w", n][:], w_raw[:, :, n : n + HC].rearrange("p j n -> p n j"))
+        def copy_on(engine, out, in_):
+            if engine == "S":
+                nc.scalar.copy(out=out, in_=in_)
+            else:
+                nc.vector.tensor_copy(out=out, in_=in_)
 
-        def w_quant(n):
-            quantize(wgs["w", n][:], w_c[:, n : n + HC], w_s[:, n : n + HC])
-
-        def v_copy(e, n, engine):
-            wgs[e, n] = sb([P, HC, J], BF16, "wg", 3)
-            copy_on(engine, wgs[e, n][:], v_raw[e][:, :, n : n + HC].rearrange("p j n -> p n j"))
-
-        def v_quant(e, n):
-            quantize(wgs[e, n][:], v_c[:, e, n : n + HC], v_s[:, e, n : n + HC])
-
-        xgs = {}
-
-        def x_turn(g, h, engine):
-            if h == 0:
-                xgs["x", g] = sb([P, KP, J], BF16, "xg", 3)
-            turn([x_raw[g][:, 2 * h + i, :] for i in range(2)], 0, xgs["x", g][:, 2 * h * P : 2 * (h + 1) * P, :], engine)
-
-        def x_quant(g):
-            quantize(xgs["x", g][:], x_c[:, g, :], x_s[:, g, :])
-
-        def e_turn(g, e, h, engine):
-            if h == 0:
-                xgs[e, g] = sb([P, KP, J], BF16, "xg", 3)
-            turn([e_raw[g][:, 2 * h + i, :] for i in range(2)], e * KP, xgs[e, g][:, 2 * h * P : 2 * (h + 1) * P, :], engine)
-
-        def e_quant(g, e):
-            quantize(xgs[e, g][:], e_c[:, g, e, :], e_s[:, g, e, :])
-
-        prods, ags = {}, {}
-
-        def product(g, t):
-            pr = sb([P, T], BF16, "prod", 6)
-            nc.vector.tensor_tensor(out=pr[:], in0=a_raw[g, t // 2][:, t % 2, :].bitcast(F8), in1=asc[:], op=MULT)
-            prods[g, t] = pr
-
-        def a_turn(g, h, q, engine):
-            if h == 0:
-                ags[g, q] = sb([P, KP, J], BF16, "ag", 5)
-            turn([prods[g, 2 * h + i][:] for i in range(2)], q * KP, ags[g, q][:, 2 * h * P : 2 * (h + 1) * P, :], engine)
-
-        def a_quant(g, q):
-            quantize(ags[g, q][:], a_c[:, g, q, :], a_s[:, g, q, :])
+        def quantize(grouped, codes, scales):
+            nc.vector.quantize_mx(out=codes.bitcast(F8X4), scales=scales, in_=grouped.rearrange("p n j -> p (n j)"))
 
         def mm(bank, pairs):
             for i, (l, ls, r, rs) in enumerate(pairs):
@@ -213,230 +447,270 @@ def tile_noise_conditioned_score_f4_kernel(tc, x, sigma, emb, w, b, v, vb, d, a_
                 )
 
         units = [(g, m) for hf in range(2) for g in range(G) for m in (2 * hf, 2 * hf + 1)]
-        st = {}
 
-        def u_mx(n):
-            g, m = units[n]
-            cs = slice(m * P, (m + 1) * P)
-            bs = slice(C + m * P, C + (m + 1) * P)
-            st["p", n], st["g", n], st["b", n] = ps("acc", 4), ps("acc", 4), ps("acc", 4)
-            mm(st["p", n][:], [(w_c[:, cs], w_s[:, cs], x_c[:, g, :], x_s[:, g, :])])
-            for nm, s_ in (("g", cs), ("b", bs)):
-                mm(st[nm, n][:], [(v_c[:, e, s_], v_s[:, e, s_], e_c[:, g, e, :], e_s[:, g, e, :]) for e in range(2)])
+        def f_d(kind, i=0, h=0):
+            if kind == "x":
+                st["x", i] = sb([P, J, C], BF16, "x_raw", 2)
+                nc.sync.dma_start(out=st["x", i][:], in_=x_v[i])
+            elif kind == "w":
+                nc.sync.dma_start(out=w_raw[:], in_=w.rearrange("(p j) n -> p j n", j=J))
+            elif kind == "e":
+                if h == 0:
+                    st["e", i] = sb([P, J, E], BF16, "e_raw", 2)
+                nc.sync.dma_start(out=st["e", i][:, 2 * h : 2 * h + 2, :], in_=e_v[i][:, 2 * h : 2 * h + 2, :])
+            elif kind == "v":
+                st["v", i] = sb([P, J, 2 * C], BF16, "k8", 3)
+                nc.sync.dma_start(out=st["v", i][:], in_=v_v[i])
+            elif kind == "a":
+                st["a", i, h] = sb([P, 2, T], U8, "a_raw", 4)
+                nc.sync.dma_start(out=st["a", i, h][:], in_=a_v[i][:, 2 * h : 2 * h + 2, :])
+            else:
+                nc.sync.dma_start(out=asc[:], in_=a_scale.rearrange("o k -> (o k)").partition_broadcast(P))
 
-        def u_hp(n):
-            g, m = units[n]
-            st["hp", n] = sb([P, KP], F32, "hp", 2)
-            nc.vector.tensor_mul(out=st["hp", n][:], in0=st["p", n][:], in1=r_t[:, g, :])
+        def f_sq():
+            nc.vector.tensor_copy(out=sig[:], in_=flat("sigma"))
+            nc.vector.tensor_mul(out=sq[:], in0=sig[:], in1=sig[:])
+            nc.vector.reciprocal(out=rsig[:], in_=sig[:])
 
-        def u_h(n):
-            g, m = units[n]
-            st["h", n] = sb([P, KP], F32, "h", 2)
-            nc.scalar.activation(out=st["h", n][:], in_=st["hp", n][:], func=ACT.Identity, bias=cols[:, m : m + 1])
-            if m % 2 == 0:
-                st["kh", g, m // 2] = sb([P, 2, KP], F32, "kh", 2)
-            nc.gpsimd.tensor_scalar(
-                out=st["kh", g, m // 2][:, m % 2, :], in0=st["hp", n][:],
-                scalar1=cols[:, m : m + 1], scalar2=cols[:, 12 + m : 13 + m], op0=ADD, op1=MULT,
+        def f_sqrt():
+            nc.scalar.activation(out=rt[:], in_=sq[:], func=ACT.Sqrt, bias=1.0)
+
+        def f_rec():
+            nc.vector.reciprocal(out=r12[:], in_=rt[:])
+
+        def f_silud():
+            nc.scalar.activation(out=dummy[:], in_=rt[:, 0:1], func=ACT.Silu)
+
+        def f_cols1():
+            nc.vector.tensor_copy(out=rows32[:], in_=rows[:])
+            nc.vector.tensor_copy(out=d4[:], in_=flat("d"))
+            nc.vector.tensor_copy(out=c4[:], in_=flat("c"))
+
+        def f_colsT():
+            st["cps"] = ps("tb")
+            nc.tensor.transpose(st["cps"][:, 0:P], rows32[:], ident[:])
+
+        def f_cols2():
+            nc.vector.tensor_copy(out=cols[:], in_=st["cps"][:, 0:16])
+            nc.vector.tensor_mul(out=crs[:], in0=c4[:], in1=rsig[:])
+            nc.vector.tensor_scalar_add(out=g1[:], in0=cols[:, 4:8], scalar1=1.0)
+
+        def f_sp(bk):
+            st["sp", bk] = ps("tb")
+            for q in range(J):
+                col = bk * J + q
+                nc.tensor.matmul(
+                    st["sp", bk][:, q * P : (q + 1) * P], lhsT=asv[:, col : col + 1].to_broadcast([P, P]), rhs=ident[:],
+                    start=True, stop=True,
+                )
+
+        def f_spc(bk):
+            nc.scalar.copy(
+                out=asc[:, bk * KP : (bk + 1) * KP].rearrange("m (p q) -> m p q", q=J),
+                in_=st["sp", bk][:].rearrange("m (q p) -> m p q", q=J),
             )
 
-        def u_z0(n):
+        def f_wcp(hf):
+            n = hf * HC
+            st["wg", hf] = sb([P, HC, J], BF16, "wg", 3)
+            copy_on("V", st["wg", hf][:], w_raw[:, :, n : n + HC].rearrange("p j n -> p n j"))
+
+        def f_wq(hf):
+            n = hf * HC
+            quantize(st["wg", hf][:], w_c[:, n : n + HC], w_s[:, n : n + HC])
+
+        def f_vcp(hf, e, i):
+            n = hf * HC + i * C
+            st["vg", hf, e, i] = sb([P, HC, J], BF16, "wg", 3)
+            copy_on("S" if (hf, e, i) in VS else "V", st["vg", hf, e, i][:], st["v", e][:, :, n : n + HC].rearrange("p j n -> p n j"))
+
+        def f_vq(hf, e, i):
+            n = hf * HC + i * C
+            quantize(st["vg", hf, e, i][:], v_c[:, e, n : n + HC], v_s[:, e, n : n + HC])
+
+        def f_turn(kind, g, q, h):
+            if kind == "a":
+                src = [st["pr", g, 2 * h + i][:] for i in range(2)]
+            else:
+                src = [st[kind, g][:, 2 * h + i, :] for i in range(2)]
+            bank = ps("tb")
+            st["tb", kind, g, q, h] = bank
+            bv = bank[:].rearrange("p (i u r) -> p i u r", i=2, u=2)
+            for i in range(2):
+                words = src[i].bitcast(F32)
+                for u in range(2):
+                    nc.tensor.transpose(bv[:, i, u, :], words[:, q * 256 + u : (q + 1) * 256 : 2], ident[:])
+
+        def f_cp(kind, g, q, h):
+            if h == FIRST[kind, g, q]:
+                st["gr", kind, g, q] = sb([P, KP, J], BF16, "ag" if kind == "a" else "xg", 5 if kind == "a" else 3)
+            dst = st["gr", kind, g, q][:, 2 * h * P : 2 * (h + 1) * P, :].rearrange("p n j -> p (n j)").bitcast(F32)
+            bv = st["tb", kind, g, q, h][:].rearrange("p (i u r) -> p i r u", i=2, u=2)
+            nc.scalar.copy(out=dst.rearrange("p (i r u) -> p i r u", i=2, u=2), in_=bv)
+
+        def f_xq(g):
+            quantize(st["gr", "x", g, 0][:], x_c[:, g, :], x_s[:, g, :])
+
+        def f_eq(g, e):
+            quantize(st["gr", "e", g, e][:], e_c[:, g, e, :], e_s[:, g, e, :])
+
+        def f_aq(g, q):
+            quantize(st["gr", "a", g, q][:], a_c[:, g, q, :], a_s[:, g, q, :])
+
+        def f_prod(g, t):
+            st["pr", g, t] = sb([P, T], BF16, "prod", 6)
+            nc.vector.tensor_tensor(out=st["pr", g, t][:], in0=st["a", g, t // 2][:, t % 2, :].bitcast(F8), in1=asc[:], op=MULT)
+
+        def f_hmx(g, hf):
+            cs = slice(hf * HC, (hf + 1) * HC)
+            for tp in range(2):
+                bank = ps("acc")
+                st["p", g, hf, tp] = bank
+                for i in range(2):
+                    ts_ = slice((2 * tp + i) * P, (2 * tp + i + 1) * P)
+                    mm(bank[:, i * HC : (i + 1) * HC], [(x_c[:, g, ts_], x_s[:, g, ts_], w_c[:, cs], w_s[:, cs])])
+
+        def f_hr(g, hf, tp):
+            if ("hr", g, hf) not in st:
+                st["hr", g, hf] = sb([P, J, HC], F32, "hr", 2)
+            for i in range(2):
+                t = 2 * tp + i
+                nc.scalar.activation(
+                    out=st["hr", g, hf][:, t, :], in_=st["p", g, hf, tp][:, i * HC : (i + 1) * HC],
+                    func=ACT.Copy, scale=r12[:, g * J + t : g * J + t + 1],
+                )
+
+        def v_mx(nm, n, c0):
             g, m = units[n]
+            s_ = slice(c0 + m * P, c0 + (m + 1) * P)
+            st[nm, n] = ps("acc")
+            mm(st[nm, n][:], [(v_c[:, e, s_], v_s[:, e, s_], e_c[:, g, e, :], e_s[:, g, e, :]) for e in range(2)])
+
+        def f_gmx(n):
+            v_mx("g", n, 0)
+
+        def f_bmx(n):
+            v_mx("b", n, C)
+
+        def f_t3(n):
+            g, m = units[n]
+            i = m % 2
+            st["ht", n] = ps("tb")
+            for t in range(J):
+                nc.tensor.transpose(st["ht", n][:, t * P : (t + 1) * P], st["hr", g, m // 2][:, t, i * P : (i + 1) * P], ident[:])
+
+        def f_h(n):
+            m = units[n][1]
+            st["h", n] = sb([P, KP], F32, "h", 2)
+            nc.scalar.activation(out=st["h", n][:], in_=st["ht", n][:], func=ACT.Identity, bias=cols[:, m : m + 1])
+
+        def f_kh(n):
+            g, m = units[n]
+            if ("kh", g, m // 2) not in st:
+                st["kh", g, m // 2] = sb([P, 2, KP], F32, "kh", 2)
+            nc.gpsimd.tensor_scalar(
+                out=st["kh", g, m // 2][:, m % 2, :], in0=st["h", n][:],
+                scalar1=cols[:, 12 + m : 13 + m], scalar2=0.0, op0=MULT, op1=ADD,
+            )
+
+        def f_z0(n):
+            m = units[n][1]
             st["z0", n] = sb([P, KP], F32, "z0", 2)
             nc.vector.scalar_tensor_tensor(
                 out=st["z0", n][:], in0=st["g", n][:], scalar=g1[:, m : m + 1], in1=st["h", n][:], op0=ADD, op1=MULT
             )
 
-        def u_z(n):
-            g, m = units[n]
-            st["z", n] = sb([P, KP], F32, "z", 2)
-            if n in ZG:
-                bt = sb([P, KP], F32, "bt", 2)
-                nc.scalar.activation(out=bt[:], in_=st["b", n][:], func=ACT.Identity, bias=cols[:, 8 + m : 9 + m])
-                nc.gpsimd.tensor_tensor(out=st["z", n][:], in0=bt[:], in1=st["z0", n][:], op=ADD)
-                return
-            nc.vector.scalar_tensor_tensor(
-                out=st["z", n][:], in0=st["b", n][:], scalar=cols[:, 8 + m : 9 + m], in1=st["z0", n][:], op0=ADD, op1=ADD
-            )
+        def f_bt(n):
+            m = units[n][1]
+            st["bt", n] = sb([P, KP], F32, "bt", 2)
+            if n in ZV:
+                nc.vector.scalar_tensor_tensor(
+                    out=st["bt", n][:], in0=st["b", n][:], scalar=cols[:, 8 + m : 9 + m], in1=st["z0", n][:], op0=ADD, op1=ADD
+                )
+            else:
+                nc.scalar.activation(out=st["bt", n][:], in_=st["b", n][:], func=ACT.Identity, bias=cols[:, 8 + m : 9 + m])
 
-        def u_t1(n):
-            st["y", n] = ps("fin", 2)
+        def f_t1(n):
+            st["zt", n] = ps("tb")
+            parts = ("bt",) if n in ZV else ("z0", "bt")
             for t in range(J):
                 ts_ = slice(t * P, (t + 1) * P)
-                nc.tensor.transpose(st["y", n][:, ts_], st["z", n][:, ts_], ident[:])
+                for part in parts:
+                    nc.tensor.matmul(
+                        st["zt", n][:, ts_], lhsT=st[part, n][:, ts_], rhs=ident[:], is_transpose=True,
+                        start=(part == parts[0]), stop=(part == "bt"),
+                    )
 
-        def u_silu(n):
+        def f_silu(n):
             st["s", n] = sb([P, KP], F32, "s", 2)
-            nc.scalar.activation(out=st["s", n][:], in_=st["y", n][:], func=ACT.Silu)
+            nc.scalar.activation(out=st["s", n][:], in_=st["zt", n][:], func=ACT.Silu)
 
-        def u_y(n):
+        def f_y(n):
             g, m = units[n]
-            if m % 2 == 0:
+            if ("yg", g, m // 2) not in st:
                 st["yg", g, m // 2] = sb([P, HC, J], BF16, "yg", 2)
             i = m % 2
-            nc.gpsimd.tensor_tensor(
+            nc.vector.tensor_tensor(
                 out=st["yg", g, m // 2][:, i * P : (i + 1) * P, :],
                 in0=st["s", n][:].rearrange("p (t c) -> p c t", t=J),
                 in1=d4[:, g * J : (g + 1) * J].unsqueeze(1).to_broadcast([P, P, J]),
                 op=MULT,
             )
 
-        def y_quant(g, hf):
+        def f_yq(g, hf):
             cs = slice(hf * HC, (hf + 1) * HC)
             quantize(st["yg", g, hf][:], y_c[:, g, cs], y_s[:, g, cs])
 
-        u_t = {}
-
-        def skip(g, hf, tp):
+        def f_t2(g, hf, tp):
             kh = st["kh", g, hf]
-            bank = ps("fin", 2)
+            bank = ps("tb")
+            st["kt", g, hf, tp] = bank
             for i in range(2):
                 for m in range(2):
                     t = 2 * tp + i
                     nc.tensor.transpose(bank[:, (2 * i + m) * P : (2 * i + m + 1) * P], kh[:, m, t * P : (t + 1) * P], ident[:])
-            if g not in u_t:
-                u_t[g] = sb([P, J, C], F32, "k8", 3)
+
+        def f_u(g, hf, tp):
+            if ("u", g) not in st:
+                st["u", g] = sb([P, J, C], F32, "k8", 3)
             for i in range(2):
-                col = g * J + 2 * tp + i
+                t = 2 * tp + i
+                col = g * J + t
                 nc.scalar.activation(
-                    out=u_t[g][:, 2 * tp + i, hf * HC : (hf + 1) * HC], in_=bank[:, i * HC : (i + 1) * HC],
+                    out=st["u", g][:, t, hf * HC : (hf + 1) * HC], in_=st["kt", g, hf, tp][:, i * HC : (i + 1) * HC],
                     func=ACT.Identity, scale=rsig[:, col : col + 1], bias=crs[:, col : col + 1],
                 )
 
-        o_v = out.rearrange("(g p t) n -> g p t n", g=G, p=P)
-
-        def o_mx(g, hf, tp):
-            bank = ps("acc", 4)
+        def f_omx(g, hf, tp):
+            bank = ps("acc" if hf and tp else "tb")
             st["o", g, hf, tp] = bank
             cs = slice(hf * HC, (hf + 1) * HC)
             for i in range(2):
                 ts_ = slice((2 * tp + i) * P, (2 * tp + i + 1) * P)
                 mm(bank[:, i * HC : (i + 1) * HC], [(a_c[:, g, q, ts_], a_s[:, g, q, ts_], y_c[:, q, cs], y_s[:, q, cs]) for q in range(G)])
 
-        def o_fin(g, hf, tp):
-            bank = st["o", g, hf, tp]
+        def f_ofin(g, hf, tp):
             cs = slice(hf * HC, (hf + 1) * HC)
+            ut = st["u", g]
             for i in range(2):
                 t = 2 * tp + i
                 col = g * J + t
                 nc.vector.scalar_tensor_tensor(
-                    out=u_t[g][:, t, cs], in0=bank[:, i * HC : (i + 1) * HC], scalar=rsig[:, col : col + 1],
-                    in1=u_t[g][:, t, cs], op0=MULT, op1=ADD,
+                    out=ut[:, t, cs], in0=st["o", g, hf, tp][:, i * HC : (i + 1) * HC], scalar=rsig[:, col : col + 1],
+                    in1=ut[:, t, cs], op0=MULT, op1=ADD,
                 )
+            nc.sync.dma_start(out=o_v[g][:, 2 * tp : 2 * tp + 2, cs], in_=ut[:, 2 * tp : 2 * tp + 2, cs])
 
-        def o_store(g, hf, tp, n):
-            cs = slice(hf * HC, (hf + 1) * HC)
-            nc.sync.dma_start(out=o_v[g][:, 2 * tp : 2 * tp + 2 * n, cs], in_=u_t[g][:, 2 * tp : 2 * tp + 2 * n, cs])
-
-        head_vec()
-        w_copy(0, "v")
-        w_quant(0)
-        head_vec2()
-        for h in range(2):
-            x_turn(0, h, "s")
-        x_quant(0)
-        spread_r(0)
-        for e in range(2):
-            for h in range(2):
-                e_turn(0, e, h, "s")
-        product(0, 0)
-        e_quant(0, 0)
-        e_quant(0, 1)
-        v_copy(0, 0, "s")
-        v_copy(0, C, "s")
-        product(0, 1)
-        v_quant(0, 0)
-        v_quant(0, C)
-        v_copy(1, 0, "v")
-        v_copy(1, C, "s")
-        v_quant(1, 0)
-        v_quant(1, C)
-        spread_r(1)
-        spread_r(2)
-        load_a(1, 1)
-        load_x(2)
-        load_e(2)
-        load_a(2, 0)
-        load_a(2, 1)
-
-        N = len(units)
-        late_w = [("v", 0, HC), ("v", 0, C + HC), ("v", 1, HC), ("v", 1, C + HC), ("w", 0, HC)]
-        a_jobs = [(g, h, q) for g in range(G) for h in range(2) for q in range(G)]
-        a_next = 0
-        p_next = 2
-        for n in range(N + 1):
-            if n < N:
-                u_mx(n)
-                u_hp(n)
-                u_h(n)
-            if n > 0:
-                u_t1(n - 1)
-                u_silu(n - 1)
-                u_y(n - 1)
-            if 2 <= n and n % 2 == 0:
-                g, m = units[n - 2]
-                for tp in range(2):
-                    skip(g, m // 2, tp)
-            if n < len(late_w):
-                nm, e, c0 = late_w[n]
-                if nm == "v":
-                    v_copy(e, c0, "s")
-                else:
-                    w_copy(c0, "s")
-            if n < 4:
-                g = 1 + n // 2
-                if n % 2 == 0:
-                    x_turn(g, 0, "s")
-                    x_turn(g, 1, "s")
-                    e_turn(g, 0, 0, "s")
-                else:
-                    e_turn(g, 0, 1, "s")
-                    e_turn(g, 1, 0, "s")
-                    e_turn(g, 1, 1, "s")
-            if p_next < 12 and n < N:
-                product(p_next // 4, p_next % 4)
-                p_next += 1
-            if n < 4:
-                g = 1 + n // 2
-                if n % 2 == 0:
-                    x_quant(g)
-                else:
-                    e_quant(g, 0)
-                    e_quant(g, 1)
-            if n < N:
-                u_z0(n)
-                u_z(n)
-            na = 1 if n < 4 else 2
-            for i in range(na):
-                if a_next < len(a_jobs):
-                    g, h, q = a_jobs[a_next]
-                    a_turn(g, h, q, "v" if n < AV else "s")
-                    a_next += 1
-                    if h == 1:
-                        a_quant(g, q)
-            if n < len(late_w):
-                nm, e, c0 = late_w[n]
-                if nm == "v":
-                    v_quant(e, c0)
-                else:
-                    w_quant(c0)
-            if n >= 2 and n % 2 == 0:
-                g, m = units[n - 2]
-                y_quant(g, m // 2)
-            if n == 8 or n == 9 or n == 10 or n == 11:
-                pass
-        while a_next < len(a_jobs):
-            g, h, q = a_jobs[a_next]
-            a_turn(g, h, q, "s")
-            a_next += 1
-            if h == 1:
-                a_quant(g, q)
-        for hf in range(2):
-            for g in range(G):
-                for tp in range(2):
-                    o_mx(g, hf, tp)
-                    o_fin(g, hf, tp)
-                    if hf:
-                        o_store(g, hf, tp, 1)
-                if not hf:
-                    o_store(g, hf, 0, 2)
+        steps = {
+            "d": f_d, "sq": f_sq, "sqrt": f_sqrt, "rec": f_rec, "silud": f_silud, "cols1": f_cols1, "colsT": f_colsT,
+            "cols2": f_cols2, "sp": f_sp, "spc": f_spc, "wcp": f_wcp, "wq": f_wq, "vcp": f_vcp, "vq": f_vq, "turn": f_turn,
+            "cp": f_cp, "xq": f_xq, "eq": f_eq, "aq": f_aq, "prod": f_prod, "hmx": f_hmx, "hr": f_hr, "gmx": f_gmx,
+            "bmx": f_bmx, "t3": f_t3, "h": f_h, "kh": f_kh, "z0": f_z0, "bt": f_bt, "t1": f_t1, "silu": f_silu, "y": f_y,
+            "yq": f_yq, "t2": f_t2, "u": f_u, "omx": f_omx, "ofin": f_ofin,
+        }
+        FIRST = {}
+        for stp in ORDER:
+            if stp[0] == "cp":
+                FIRST.setdefault(stp[1:4], stp[4])
+        for stp in ORDER:
+            steps[stp[0]](*stp[1:])

@@ -22,334 +22,334 @@ KP = P * J
 G = T // KP
 M = C // P
 HC = C // 2
-ZV = ()
+ZV = (1, 3, 5, 7, 9, 11)
 VS = ((0, 1, 1),)
 ORDER = [
-    ("d", "x", 0),
-    ("d", "e", 0, 0),
-    ("d", "w"),
-    ("d", "v", 0),
     ("d", "e", 0, 1),
+    ("d", "e", 0, 0),
+    ("d", "x", 0),
+    ("d", "v", 0),
+    ("d", "w"),
+    ("d", "a", 0, 1),
     ("d", "v", 1),
     ("d", "a", 0, 0),
-    ("d", "e", 1, 0),
     ("d", "x", 1),
-    ("d", "e", 1, 1),
-    ("sq",),
-    ("sp", 1),
-    ("wcp", 0),
-    ("turn", "x", 0, 0, 1),
-    ("turn", "e", 0, 0, 0),
-    ("wq", 0),
-    ("turn", "x", 0, 0, 0),
-    ("d", "x", 2),
-    ("d", "a", 0, 1),
-    ("spc", 1),
-    ("turn", "e", 0, 1, 0),
-    ("sp", 0),
+    ("d", "e", 2, 1),
+    ("d", "a", 1, 1),
+    ("turn", "e", 0, 1, 1),
     ("cols1",),
-    ("cp", "e", 0, 0, 0),
-    ("vcp", 0, 0, 1),
+    ("sp", 0),
     ("turn", "e", 0, 0, 1),
+    ("sq",),
+    ("vcp", 0, 0, 1),
+    ("cp", "e", 0, 0, 1),
+    ("spc", 0),
+    ("turn", "x", 0, 0, 0),
+    ("turn", "e", 0, 1, 0),
     ("vcp", 0, 0, 0),
     ("vq", 0, 0, 1),
-    ("cp", "x", 0, 0, 1),
-    ("cp", "x", 0, 0, 0),
-    ("wcp", 1),
-    ("vq", 0, 0, 0),
-    ("sqrt",),
-    ("turn", "e", 0, 1, 1),
-    ("d", "e", 2, 0),
-    ("d", "e", 2, 1),
-    ("d", "a", 1, 0),
-    ("d", "a", 1, 1),
-    ("cp", "e", 0, 1, 0),
-    ("spc", 0),
-    ("cp", "e", 0, 0, 1),
-    ("xq", 0),
-    ("sp", 2),
     ("cp", "e", 0, 1, 1),
-    ("rec",),
-    ("colsT",),
-    ("wq", 1),
-    ("vcp", 0, 1, 1),
-    ("hmx", 0, 0),
+    ("wcp", 0),
+    ("vq", 0, 0, 0),
+    ("wcp", 1),
+    ("sqrt",),
+    ("turn", "e", 0, 0, 0),
+    ("d", "e", 1, 0),
+    ("d", "e", 1, 1),
+    ("d", "a", 1, 0),
+    ("d", "e", 2, 0),
+    ("turn", "x", 0, 0, 1),
+    ("d", "x", 2),
+    ("cp", "e", 0, 1, 0),
+    ("wq", 0),
+    ("cp", "x", 0, 0, 0),
+    ("cp", "x", 0, 0, 1),
+    ("sp", 1),
+    ("xq", 0),
     ("vcp", 0, 1, 0),
+    ("hmx", 0, 0),
     ("vq", 0, 1, 0),
+    ("cp", "e", 0, 0, 0),
+    ("sp", 2),
+    ("turn", "x", 1, 0, 0),
+    ("rec",),
+    ("eq", 0, 0),
+    ("eq", 0, 1),
+    ("silud",),
+    ("spc", 1),
+    ("vcp", 0, 1, 1),
+    ("vq", 0, 1, 1),
+    ("colsT",),
+    ("hr", 0, 0, 0),
+    ("wq", 1),
+    ("turn", "x", 1, 0, 1),
     ("spc", 2),
     ("hr", 0, 0, 1),
-    ("eq", 0, 1),
-    ("hr", 0, 0, 0),
-    ("eq", 0, 0),
-    ("silud",),
     ("cols2",),
-    ("vq", 0, 1, 1),
-    ("prod", 0, 0),
-    ("turn", "x", 1, 0, 0),
-    ("turn", "x", 1, 0, 1),
-    ("t3", 0),
     ("cp", "x", 1, 0, 0),
-    ("bmx", 0),
-    ("gmx", 0),
+    ("prod", 0, 0),
     ("turn", "e", 1, 0, 0),
     ("cp", "x", 1, 0, 1),
+    ("t3", 0),
     ("turn", "e", 1, 0, 1),
-    ("prod", 0, 1),
-    ("d", "a", 2, 0),
-    ("h", 0),
     ("cp", "e", 1, 0, 0),
+    ("gmx", 0),
     ("turn", "e", 1, 1, 0),
     ("xq", 1),
     ("cp", "e", 1, 0, 1),
-    ("turn", "e", 1, 1, 1),
-    ("t3", 1),
-    ("hmx", 1, 0),
-    ("bt", 0),
-    ("z0", 0),
-    ("bmx", 1),
+    ("prod", 0, 1),
+    ("h", 0),
     ("kh", 0),
-    ("gmx", 1),
+    ("turn", "e", 1, 1, 1),
+    ("bmx", 0),
+    ("z0", 0),
     ("cp", "e", 1, 1, 0),
-    ("turn", "x", 2, 0, 0),
+    ("t3", 1),
     ("vcp", 1, 0, 0),
-    ("eq", 1, 0),
+    ("turn", "x", 2, 0, 0),
     ("vq", 1, 0, 0),
+    ("bt", 0),
+    ("gmx", 1),
+    ("eq", 1, 0),
     ("cp", "e", 1, 1, 1),
-    ("hr", 1, 0, 0),
-    ("hr", 1, 0, 1),
     ("turn", "x", 2, 0, 1),
+    ("hmx", 1, 0),
+    ("cp", "x", 2, 0, 0),
     ("prod", 0, 2),
     ("h", 1),
+    ("kh", 1),
+    ("bmx", 1),
     ("t1", 0),
-    ("cp", "x", 2, 0, 0),
     ("turn", "e", 2, 0, 0),
+    ("z0", 1),
+    ("hr", 1, 0, 0),
+    ("hr", 1, 0, 1),
+    ("t3", 2),
     ("eq", 1, 1),
     ("cp", "x", 2, 0, 1),
-    ("turn", "e", 2, 0, 1),
-    ("t3", 2),
     ("vcp", 1, 0, 1),
-    ("bt", 1),
-    ("z0", 1),
-    ("bmx", 2),
-    ("vq", 1, 0, 1),
-    ("kh", 1),
-    ("gmx", 2),
-    ("t2", 0, 0, 0),
-    ("cp", "e", 2, 0, 0),
-    ("turn", "e", 2, 1, 0),
-    ("t2", 0, 0, 1),
-    ("xq", 2),
     ("silu", 0),
-    ("cp", "e", 2, 0, 1),
+    ("vq", 1, 0, 1),
+    ("turn", "e", 2, 0, 1),
+    ("bt", 1),
+    ("gmx", 2),
+    ("cp", "e", 2, 0, 0),
+    ("turn", "a", 0, 0, 0),
+    ("turn", "e", 2, 1, 0),
+    ("t2", 0, 0, 0),
     ("h", 2),
+    ("kh", 2),
+    ("xq", 2),
+    ("cp", "e", 2, 0, 1),
     ("prod", 0, 3),
     ("d", "a", 2, 1),
-    ("turn", "e", 2, 1, 1),
-    ("u", 0, 0, 0),
+    ("d", "a", 2, 0),
+    ("bmx", 2),
     ("t1", 1),
+    ("z0", 2),
+    ("turn", "e", 2, 1, 1),
+    ("t3", 3),
+    ("cp", "a", 0, 0, 0),
+    ("u", 0, 0, 0),
     ("cp", "e", 2, 1, 0),
-    ("u", 0, 0, 1),
+    ("silu", 1),
+    ("turn", "a", 0, 1, 0),
     ("vcp", 1, 1, 0),
+    ("y", 0),
+    ("bt", 2),
+    ("gmx", 3),
     ("vq", 1, 1, 0),
     ("eq", 2, 0),
     ("cp", "e", 2, 1, 1),
-    ("t3", 3),
     ("hmx", 2, 0),
-    ("bt", 2),
-    ("z0", 2),
-    ("turn", "a", 0, 0, 0),
+    ("cp", "a", 0, 1, 0),
+    ("h", 3),
+    ("kh", 3),
     ("bmx", 3),
-    ("kh", 2),
-    ("gmx", 3),
-    ("eq", 2, 1),
-    ("silu", 1),
+    ("t1", 2),
+    ("turn", "a", 0, 2, 0),
+    ("t2", 0, 0, 1),
+    ("prod", 1, 0),
+    ("z0", 3),
     ("hr", 2, 0, 0),
     ("hr", 2, 0, 1),
-    ("y", 0),
-    ("h", 3),
-    ("prod", 1, 0),
-    ("vcp", 1, 1, 1),
-    ("cp", "a", 0, 0, 0),
-    ("t1", 2),
-    ("vq", 1, 1, 1),
-    ("turn", "a", 0, 1, 0),
     ("t3", 4),
-    ("bt", 3),
-    ("z0", 3),
-    ("bmx", 4),
-    ("cp", "a", 0, 1, 0),
-    ("kh", 3),
-    ("gmx", 4),
-    ("t2", 1, 0, 0),
-    ("turn", "a", 0, 2, 0),
-    ("t2", 1, 0, 1),
     ("silu", 2),
+    ("eq", 2, 1),
     ("y", 1),
-    ("h", 4),
-    ("prod", 1, 1),
-    ("u", 1, 0, 0),
-    ("t1", 3),
+    ("bt", 3),
+    ("gmx", 4),
+    ("vcp", 1, 1, 1),
     ("cp", "a", 0, 2, 0),
+    ("vq", 1, 1, 1),
+    ("u", 0, 0, 1),
     ("turn", "a", 0, 0, 1),
-    ("u", 1, 0, 1),
-    ("t3", 5),
-    ("hmx", 0, 1),
-    ("bt", 4),
-    ("z0", 4),
-    ("bmx", 5),
+    ("t2", 1, 0, 0),
+    ("h", 4),
     ("kh", 4),
-    ("gmx", 5),
+    ("bmx", 4),
+    ("t1", 3),
+    ("z0", 4),
+    ("prod", 1, 1),
+    ("t3", 5),
     ("cp", "a", 0, 0, 1),
-    ("turn", "a", 0, 1, 1),
+    ("u", 1, 0, 0),
     ("silu", 3),
+    ("turn", "a", 0, 1, 1),
+    ("yq", 0, 0),
+    ("y", 2),
+    ("bt", 4),
+    ("gmx", 5),
+    ("hmx", 0, 1),
+    ("cp", "a", 0, 1, 1),
+    ("h", 5),
+    ("kh", 5),
+    ("bmx", 5),
+    ("aq", 0, 0),
+    ("t1", 4),
+    ("turn", "a", 0, 2, 1),
+    ("t2", 1, 0, 1),
+    ("z0", 5),
     ("hr", 0, 1, 0),
     ("hr", 0, 1, 1),
-    ("y", 2),
-    ("h", 5),
-    ("prod", 1, 2),
-    ("t1", 4),
-    ("cp", "a", 0, 1, 1),
-    ("turn", "a", 0, 2, 1),
     ("t3", 6),
-    ("bt", 5),
-    ("z0", 5),
-    ("bmx", 6),
-    ("kh", 5),
-    ("gmx", 6),
-    ("t2", 2, 0, 0),
-    ("cp", "a", 0, 2, 1),
-    ("t2", 2, 0, 1),
-    ("turn", "a", 1, 0, 0),
+    ("prod", 1, 2),
     ("silu", 4),
     ("y", 3),
-    ("h", 6),
-    ("aq", 0, 0),
-    ("u", 2, 0, 0),
-    ("prod", 1, 3),
-    ("t1", 5),
-    ("u", 2, 0, 1),
-    ("cp", "a", 1, 0, 0),
-    ("turn", "a", 1, 1, 0),
-    ("yq", 0, 0),
-    ("t3", 7),
-    ("hmx", 1, 1),
-    ("bt", 6),
-    ("z0", 6),
+    ("bt", 5),
+    ("gmx", 6),
+    ("cp", "a", 0, 2, 1),
+    ("u", 1, 0, 1),
     ("aq", 0, 1),
-    ("bmx", 7),
+    ("turn", "a", 1, 0, 0),
+    ("t2", 2, 0, 0),
+    ("h", 6),
     ("kh", 6),
-    ("gmx", 7),
-    ("cp", "a", 1, 1, 0),
-    ("turn", "a", 1, 2, 0),
+    ("bmx", 6),
+    ("t1", 5),
+    ("z0", 6),
+    ("t3", 7),
+    ("cp", "a", 1, 0, 0),
+    ("prod", 1, 3),
+    ("u", 2, 0, 0),
+    ("aq", 0, 2),
     ("silu", 5),
+    ("turn", "a", 1, 1, 0),
+    ("yq", 1, 0),
+    ("y", 4),
+    ("bt", 6),
+    ("gmx", 7),
+    ("hmx", 1, 1),
+    ("cp", "a", 1, 1, 0),
+    ("h", 7),
+    ("kh", 7),
+    ("bmx", 7),
+    ("t1", 6),
+    ("turn", "a", 1, 2, 0),
+    ("t2", 2, 0, 1),
+    ("z0", 7),
     ("hr", 1, 1, 0),
     ("hr", 1, 1, 1),
-    ("y", 4),
-    ("h", 7),
-    ("t1", 6),
-    ("prod", 2, 0),
-    ("aq", 0, 2),
-    ("cp", "a", 1, 2, 0),
-    ("turn", "a", 1, 0, 1),
     ("t3", 8),
-    ("bt", 7),
-    ("z0", 7),
-    ("bmx", 8),
-    ("kh", 7),
-    ("gmx", 8),
-    ("t2", 0, 1, 0),
-    ("t2", 0, 1, 1),
-    ("cp", "a", 1, 0, 1),
-    ("turn", "a", 1, 1, 1),
     ("silu", 6),
+    ("prod", 2, 0),
     ("y", 5),
+    ("bt", 7),
+    ("gmx", 8),
+    ("cp", "a", 1, 2, 0),
+    ("u", 2, 0, 1),
+    ("turn", "a", 1, 0, 1),
+    ("t2", 0, 1, 0),
     ("h", 8),
-    ("u", 0, 1, 0),
-    ("t1", 7),
-    ("prod", 2, 1),
-    ("u", 0, 1, 1),
-    ("cp", "a", 1, 1, 1),
-    ("turn", "a", 1, 2, 1),
-    ("yq", 1, 0),
-    ("t3", 9),
-    ("hmx", 2, 1),
-    ("bt", 8),
-    ("z0", 8),
-    ("bmx", 9),
     ("kh", 8),
-    ("gmx", 9),
-    ("cp", "a", 1, 2, 1),
+    ("bmx", 8),
+    ("t1", 7),
+    ("z0", 8),
+    ("t3", 9),
+    ("cp", "a", 1, 0, 1),
+    ("u", 0, 1, 0),
     ("silu", 7),
+    ("turn", "a", 1, 1, 1),
+    ("yq", 2, 0),
+    ("y", 6),
+    ("bt", 8),
+    ("prod", 2, 1),
+    ("gmx", 9),
+    ("hmx", 2, 1),
+    ("cp", "a", 1, 1, 1),
+    ("h", 9),
+    ("kh", 9),
+    ("bmx", 9),
+    ("aq", 1, 0),
+    ("t1", 8),
+    ("turn", "a", 1, 2, 1),
+    ("t2", 0, 1, 1),
+    ("z0", 9),
     ("hr", 2, 1, 0),
     ("hr", 2, 1, 1),
-    ("y", 6),
-    ("turn", "a", 2, 0, 0),
-    ("h", 9),
-    ("t1", 8),
-    ("prod", 2, 2),
-    ("aq", 1, 0),
-    ("cp", "a", 2, 0, 0),
-    ("turn", "a", 2, 1, 0),
     ("t3", 10),
-    ("bt", 9),
-    ("z0", 9),
-    ("bmx", 10),
-    ("kh", 9),
-    ("gmx", 10),
-    ("t2", 1, 1, 0),
-    ("aq", 1, 1),
-    ("t2", 1, 1, 1),
     ("silu", 8),
     ("y", 7),
-    ("cp", "a", 2, 1, 0),
+    ("bt", 9),
+    ("gmx", 10),
+    ("cp", "a", 1, 2, 1),
+    ("prod", 2, 2),
+    ("u", 0, 1, 1),
+    ("aq", 1, 1),
+    ("turn", "a", 2, 0, 0),
+    ("t2", 1, 1, 0),
     ("h", 10),
-    ("turn", "a", 2, 2, 0),
-    ("u", 1, 1, 0),
-    ("t1", 9),
-    ("prod", 2, 3),
-    ("u", 1, 1, 1),
-    ("aq", 1, 2),
-    ("yq", 2, 0),
-    ("t3", 11),
-    ("cp", "a", 2, 2, 0),
-    ("turn", "a", 2, 0, 1),
-    ("bt", 10),
-    ("z0", 10),
-    ("bmx", 11),
     ("kh", 10),
-    ("gmx", 11),
+    ("bmx", 10),
+    ("t1", 9),
+    ("z0", 10),
+    ("t3", 11),
+    ("cp", "a", 2, 0, 0),
+    ("u", 1, 1, 0),
+    ("aq", 1, 2),
+    ("turn", "a", 2, 1, 0),
     ("silu", 9),
+    ("yq", 0, 1),
     ("y", 8),
+    ("bt", 10),
+    ("gmx", 11),
+    ("prod", 2, 3),
+    ("cp", "a", 2, 1, 0),
     ("h", 11),
-    ("cp", "a", 2, 0, 1),
-    ("turn", "a", 2, 1, 1),
-    ("t1", 10),
-    ("cp", "a", 2, 1, 1),
-    ("bt", 11),
-    ("z0", 11),
-    ("turn", "a", 2, 2, 1),
     ("kh", 11),
-    ("t2", 2, 1, 0),
-    ("t2", 2, 1, 1),
+    ("bmx", 11),
+    ("t1", 10),
+    ("turn", "a", 2, 2, 0),
+    ("t2", 1, 1, 1),
+    ("z0", 11),
+    ("omx", 0, 0, 0),
     ("silu", 10),
     ("y", 9),
-    ("cp", "a", 2, 2, 1),
-    ("u", 2, 1, 0),
+    ("bt", 11),
+    ("cp", "a", 2, 2, 0),
+    ("u", 1, 1, 1),
+    ("turn", "a", 2, 0, 1),
+    ("t2", 2, 1, 0),
     ("t1", 11),
-    ("u", 2, 1, 1),
-    ("aq", 2, 0),
-    ("yq", 0, 1),
-    ("aq", 2, 1),
-    ("silu", 11),
-    ("y", 10),
-    ("aq", 2, 2),
-    ("omx", 0, 0, 0),
-    ("y", 11),
     ("ofin", 0, 0, 0),
+    ("cp", "a", 2, 0, 1),
+    ("u", 2, 1, 0),
+    ("turn", "a", 2, 1, 1),
+    ("silu", 11),
     ("yq", 1, 1),
+    ("y", 10),
     ("omx", 0, 0, 1),
+    ("cp", "a", 2, 1, 1),
+    ("aq", 2, 0),
+    ("turn", "a", 2, 2, 1),
+    ("t2", 2, 1, 1),
+    ("y", 11),
     ("ofin", 0, 0, 1),
+    ("cp", "a", 2, 2, 1),
+    ("u", 2, 1, 1),
+    ("aq", 2, 1),
     ("omx", 1, 0, 0),
+    ("aq", 2, 2),
     ("yq", 2, 1),
     ("ofin", 1, 0, 0),
     ("omx", 1, 0, 1),
@@ -455,7 +455,7 @@ def tile_noise_conditioned_score_f4_kernel(tc, x, sigma, emb, w, b, v, vb, d, a_
             elif kind == "w":
                 nc.sync.dma_start(out=w_raw[:], in_=w.rearrange("(p j) n -> p j n", j=J))
             elif kind == "e":
-                if h == 0:
+                if ("e", i) not in st:
                     st["e", i] = sb([P, J, E], BF16, "e_raw", 2)
                 nc.sync.dma_start(out=st["e", i][:, 2 * h : 2 * h + 2, :], in_=e_v[i][:, 2 * h : 2 * h + 2, :])
             elif kind == "v":
@@ -499,9 +499,8 @@ def tile_noise_conditioned_score_f4_kernel(tc, x, sigma, emb, w, b, v, vb, d, a_
             st["sp", bk] = ps("tb")
             for q in range(J):
                 col = bk * J + q
-                nc.tensor.matmul(
-                    st["sp", bk][:, q * P : (q + 1) * P], lhsT=asv[:, col : col + 1].to_broadcast([P, P]), rhs=ident[:],
-                    start=True, stop=True,
+                nc.tensor.transpose(
+                    st["sp", bk][:, q * P : (q + 1) * P], asv[:, col : col + 1].to_broadcast([P, P]), ident[:]
                 )
 
         def f_spc(bk):
@@ -643,7 +642,9 @@ def tile_noise_conditioned_score_f4_kernel(tc, x, sigma, emb, w, b, v, vb, d, a_
 
         def f_silu(n):
             st["s", n] = sb([P, KP], F32, "s", 2)
-            nc.scalar.activation(out=st["s", n][:], in_=st["zt", n][:], func=ACT.Silu)
+            nc.scalar.activation(
+                out=st["s", n][:].rearrange("p (c t) -> p c t", t=J), in_=st["zt", n][:].rearrange("p (t c) -> p c t", t=J), func=ACT.Silu
+            )
 
         def f_y(n):
             g, m = units[n]
@@ -652,7 +653,7 @@ def tile_noise_conditioned_score_f4_kernel(tc, x, sigma, emb, w, b, v, vb, d, a_
             i = m % 2
             nc.vector.tensor_tensor(
                 out=st["yg", g, m // 2][:, i * P : (i + 1) * P, :],
-                in0=st["s", n][:].rearrange("p (t c) -> p c t", t=J),
+                in0=st["s", n][:].rearrange("p (c t) -> p c t", t=J),
                 in1=d4[:, g * J : (g + 1) * J].unsqueeze(1).to_broadcast([P, P, J]),
                 op=MULT,
             )

from contextlib import ExitStack

import concourse.mybir as mybir
from concourse.masks import make_identity

T, C, E = 1536, 512, 1024
FLOPS = 2 * (T * C * C + T * E * 2 * C + T * T * C)

F32 = mybir.dt.float32
BF16 = mybir.dt.bfloat16
U32 = mybir.dt.uint32
U8 = mybir.dt.uint8
F8 = mybir.dt.float8_e4m3fn
F8X4 = mybir.dt.float8_e4m3fn_x4
ACT = mybir.ActivationFunctionType
ADD = mybir.AluOpType.add
MULT = mybir.AluOpType.mult

P = 128
J = 4
KP = P * J
G = T // KP
M = C // P
HC = C // 2
ZV = (1, 3, 5, 7, 9, 11)
VS = ((0, 1, 1),)
ORDER = [
    ("d", "e", 0, 1),
    ("d", "e", 0, 0),
    ("d", "x", 0),
    ("d", "v", 0),
    ("d", "w"),
    ("d", "a", 0, 1),
    ("d", "v", 1),
    ("d", "a", 0, 0),
    ("d", "x", 1),
    ("d", "e", 2, 1),
    ("d", "a", 1, 1),
    ("turn", "e", 0, 1, 1),
    ("cols1",),
    ("sp", 0),
    ("turn", "e", 0, 0, 1),
    ("sq",),
    ("vcp", 0, 0, 1),
    ("cp", "e", 0, 0, 1),
    ("spc", 0),
    ("turn", "x", 0, 0, 0),
    ("turn", "e", 0, 1, 0),
    ("vcp", 0, 0, 0),
    ("vq", 0, 0, 1),
    ("cp", "e", 0, 1, 1),
    ("wcp", 0),
    ("vq", 0, 0, 0),
    ("wcp", 1),
    ("sqrt",),
    ("turn", "e", 0, 0, 0),
    ("d", "e", 1, 0),
    ("d", "e", 1, 1),
    ("d", "a", 1, 0),
    ("d", "e", 2, 0),
    ("turn", "x", 0, 0, 1),
    ("d", "x", 2),
    ("cp", "e", 0, 1, 0),
    ("wq", 0),
    ("cp", "x", 0, 0, 0),
    ("cp", "x", 0, 0, 1),
    ("sp", 1),
    ("xq", 0),
    ("vcp", 0, 1, 0),
    ("hmx", 0, 0),
    ("vq", 0, 1, 0),
    ("cp", "e", 0, 0, 0),
    ("sp", 2),
    ("turn", "x", 1, 0, 0),
    ("rec",),
    ("eq", 0, 0),
    ("eq", 0, 1),
    ("silud",),
    ("spc", 1),
    ("vcp", 0, 1, 1),
    ("vq", 0, 1, 1),
    ("colsT",),
    ("hr", 0, 0, 0),
    ("wq", 1),
    ("turn", "x", 1, 0, 1),
    ("spc", 2),
    ("hr", 0, 0, 1),
    ("cols2",),
    ("cp", "x", 1, 0, 0),
    ("prod", 0, 0),
    ("turn", "e", 1, 0, 0),
    ("cp", "x", 1, 0, 1),
    ("t3", 0),
    ("turn", "e", 1, 0, 1),
    ("cp", "e", 1, 0, 0),
    ("gmx", 0),
    ("turn", "e", 1, 1, 0),
    ("xq", 1),
    ("cp", "e", 1, 0, 1),
    ("prod", 0, 1),
    ("h", 0),
    ("kh", 0),
    ("turn", "e", 1, 1, 1),
    ("bmx", 0),
    ("z0", 0),
    ("cp", "e", 1, 1, 0),
    ("t3", 1),
    ("vcp", 1, 0, 0),
    ("turn", "x", 2, 0, 0),
    ("vq", 1, 0, 0),
    ("bt", 0),
    ("gmx", 1),
    ("eq", 1, 0),
    ("cp", "e", 1, 1, 1),
    ("turn", "x", 2, 0, 1),
    ("hmx", 1, 0),
    ("cp", "x", 2, 0, 0),
    ("prod", 0, 2),
    ("h", 1),
    ("kh", 1),
    ("bmx", 1),
    ("t1", 0),
    ("turn", "e", 2, 0, 0),
    ("z0", 1),
    ("hr", 1, 0, 0),
    ("hr", 1, 0, 1),
    ("t3", 2),
    ("eq", 1, 1),
    ("cp", "x", 2, 0, 1),
    ("vcp", 1, 0, 1),
    ("silu", 0),
    ("vq", 1, 0, 1),
    ("turn", "e", 2, 0, 1),
    ("bt", 1),
    ("gmx", 2),
    ("cp", "e", 2, 0, 0),
    ("turn", "a", 0, 0, 0),
    ("turn", "e", 2, 1, 0),
    ("t2", 0, 0, 0),
    ("h", 2),
    ("kh", 2),
    ("xq", 2),
    ("cp", "e", 2, 0, 1),
    ("prod", 0, 3),
    ("d", "a", 2, 1),
    ("d", "a", 2, 0),
    ("bmx", 2),
    ("t1", 1),
    ("z0", 2),
    ("turn", "e", 2, 1, 1),
    ("t3", 3),
    ("cp", "a", 0, 0, 0),
    ("u", 0, 0, 0),
    ("cp", "e", 2, 1, 0),
    ("silu", 1),
    ("turn", "a", 0, 1, 0),
    ("vcp", 1, 1, 0),
    ("y", 0),
    ("bt", 2),
    ("gmx", 3),
    ("vq", 1, 1, 0),
    ("eq", 2, 0),
    ("cp", "e", 2, 1, 1),
    ("hmx", 2, 0),
    ("cp", "a", 0, 1, 0),
    ("h", 3),
    ("kh", 3),
    ("bmx", 3),
    ("t1", 2),
    ("turn", "a", 0, 2, 0),
    ("t2", 0, 0, 1),
    ("prod", 1, 0),
    ("z0", 3),
    ("hr", 2, 0, 0),
    ("hr", 2, 0, 1),
    ("t3", 4),
    ("silu", 2),
    ("eq", 2, 1),
    ("y", 1),
    ("bt", 3),
    ("gmx", 4),
    ("vcp", 1, 1, 1),
    ("cp", "a", 0, 2, 0),
    ("vq", 1, 1, 1),
    ("u", 0, 0, 1),
    ("turn", "a", 0, 0, 1),
    ("t2", 1, 0, 0),
    ("h", 4),
    ("kh", 4),
    ("bmx", 4),
    ("t1", 3),
    ("z0", 4),
    ("prod", 1, 1),
    ("t3", 5),
    ("cp", "a", 0, 0, 1),
    ("u", 1, 0, 0),
    ("silu", 3),
    ("turn", "a", 0, 1, 1),
    ("yq", 0, 0),
    ("y", 2),
    ("bt", 4),
    ("gmx", 5),
    ("hmx", 0, 1),
    ("cp", "a", 0, 1, 1),
    ("h", 5),
    ("kh", 5),
    ("bmx", 5),
    ("aq", 0, 0),
    ("t1", 4),
    ("turn", "a", 0, 2, 1),
    ("t2", 1, 0, 1),
    ("z0", 5),
    ("hr", 0, 1, 0),
    ("hr", 0, 1, 1),
    ("t3", 6),
    ("prod", 1, 2),
    ("silu", 4),
    ("y", 3),
    ("bt", 5),
    ("gmx", 6),
    ("cp", "a", 0, 2, 1),
    ("u", 1, 0, 1),
    ("aq", 0, 1),
    ("turn", "a", 1, 0, 0),
    ("t2", 2, 0, 0),
    ("h", 6),
    ("kh", 6),
    ("bmx", 6),
    ("t1", 5),
    ("z0", 6),
    ("t3", 7),
    ("cp", "a", 1, 0, 0),
    ("prod", 1, 3),
    ("u", 2, 0, 0),
    ("aq", 0, 2),
    ("silu", 5),
    ("turn", "a", 1, 1, 0),
    ("yq", 1, 0),
    ("y", 4),
    ("bt", 6),
    ("gmx", 7),
    ("hmx", 1, 1),
    ("cp", "a", 1, 1, 0),
    ("h", 7),
    ("kh", 7),
    ("bmx", 7),
    ("t1", 6),
    ("turn", "a", 1, 2, 0),
    ("t2", 2, 0, 1),
    ("z0", 7),
    ("hr", 1, 1, 0),
    ("hr", 1, 1, 1),
    ("t3", 8),
    ("silu", 6),
    ("prod", 2, 0),
    ("y", 5),
    ("bt", 7),
    ("gmx", 8),
    ("cp", "a", 1, 2, 0),
    ("u", 2, 0, 1),
    ("turn", "a", 1, 0, 1),
    ("t2", 0, 1, 0),
    ("h", 8),
    ("kh", 8),
    ("bmx", 8),
    ("t1", 7),
    ("z0", 8),
    ("t3", 9),
    ("cp", "a", 1, 0, 1),
    ("u", 0, 1, 0),
    ("silu", 7),
    ("turn", "a", 1, 1, 1),
    ("yq", 2, 0),
    ("y", 6),
    ("bt", 8),
    ("prod", 2, 1),
    ("gmx", 9),
    ("hmx", 2, 1),
    ("cp", "a", 1, 1, 1),
    ("h", 9),
    ("kh", 9),
    ("bmx", 9),
    ("aq", 1, 0),
    ("t1", 8),
    ("turn", "a", 1, 2, 1),
    ("t2", 0, 1, 1),
    ("z0", 9),
    ("hr", 2, 1, 0),
    ("hr", 2, 1, 1),
    ("t3", 10),
    ("silu", 8),
    ("y", 7),
    ("bt", 9),
    ("gmx", 10),
    ("cp", "a", 1, 2, 1),
    ("prod", 2, 2),
    ("u", 0, 1, 1),
    ("aq", 1, 1),
    ("turn", "a", 2, 0, 0),
    ("t2", 1, 1, 0),
    ("h", 10),
    ("kh", 10),
    ("bmx", 10),
    ("t1", 9),
    ("z0", 10),
    ("t3", 11),
    ("cp", "a", 2, 0, 0),
    ("u", 1, 1, 0),
    ("aq", 1, 2),
    ("turn", "a", 2, 1, 0),
    ("silu", 9),
    ("yq", 0, 1),
    ("y", 8),
    ("bt", 10),
    ("gmx", 11),
    ("prod", 2, 3),
    ("cp", "a", 2, 1, 0),
    ("h", 11),
    ("kh", 11),
    ("bmx", 11),
    ("t1", 10),
    ("turn", "a", 2, 2, 0),
    ("t2", 1, 1, 1),
    ("z0", 11),
    ("omx", 0, 0, 0),
    ("silu", 10),
    ("y", 9),
    ("bt", 11),
    ("cp", "a", 2, 2, 0),
    ("u", 1, 1, 1),
    ("turn", "a", 2, 0, 1),
    ("t2", 2, 1, 0),
    ("t1", 11),
    ("ofin", 0, 0, 0),
    ("cp", "a", 2, 0, 1),
    ("u", 2, 1, 0),
    ("turn", "a", 2, 1, 1),
    ("silu", 11),
    ("yq", 1, 1),
    ("y", 10),
    ("omx", 0, 0, 1),
    ("cp", "a", 2, 1, 1),
    ("aq", 2, 0),
    ("turn", "a", 2, 2, 1),
    ("t2", 2, 1, 1),
    ("y", 11),
    ("ofin", 0, 0, 1),
    ("cp", "a", 2, 2, 1),
    ("u", 2, 1, 1),
    ("aq", 2, 1),
    ("omx", 1, 0, 0),
    ("aq", 2, 2),
    ("yq", 2, 1),
    ("ofin", 1, 0, 0),
    ("omx", 1, 0, 1),
    ("ofin", 1, 0, 1),
    ("omx", 2, 0, 0),
    ("ofin", 2, 0, 0),
    ("omx", 2, 0, 1),
    ("ofin", 2, 0, 1),
    ("omx", 0, 1, 0),
    ("ofin", 0, 1, 0),
    ("omx", 0, 1, 1),
    ("ofin", 0, 1, 1),
    ("omx", 1, 1, 0),
    ("ofin", 1, 1, 0),
    ("omx", 1, 1, 1),
    ("ofin", 1, 1, 1),
    ("omx", 2, 1, 0),
    ("ofin", 2, 1, 0),
    ("omx", 2, 1, 1),
    ("ofin", 2, 1, 1),
]


def tile_noise_conditioned_score_f4_kernel(tc, x, sigma, emb, w, b, v, vb, d, a_bytes, a_scale, c, k, out):
    nc = tc.nc
    with ExitStack() as ctx:
        pool = ctx.enter_context(tc.tile_pool(name="sb", bufs=1))
        psum = ctx.enter_context(tc.psum_pool(name="ps", bufs=1))
        ctx.enter_context(tc.manual_schedule())

        def sb(shape, dtype, tag, bufs=1):
            return pool.tile(shape, dtype, name=tag, tag=tag, bufs=bufs, align_bytes=64)

        def ps(tag):
            return psum.tile([P, KP], F32, name=tag, tag=tag, bufs=4)

        x_v = x.rearrange("(g p t) n -> g p t n", g=G, p=P)
        e_v = emb.rearrange("(g p t) n -> g p t n", g=G, p=P)
        a_v = a_bytes.rearrange("(g p t) n -> g p t n", g=G, p=P)
        v_v = v.rearrange("(g p j) n -> g p j n", g=2, p=P)
        o_v = out.rearrange("(g p t) n -> g p t n", g=G, p=P)
        st = {}

        tok = {}
        asv = sb([P, G * J], F32, "asv")
        for nm, vec in (("sigma", sigma), ("d", d), ("c", c)):
            tok[nm] = sb([P, G, J], BF16, "tok_" + nm)
        nc.scalar.dma_start(out=tok["sigma"][:], in_=sigma.rearrange("(g p t) -> p g t", g=G, p=P))
        nc.scalar.dma_start(
            out=asv[:].rearrange("p (g t) -> p g t", g=G), in_=a_scale.rearrange("o (g p t) -> p (o g) t", g=G, p=P)
        )
        rows = sb([P, P], BF16, "rows")
        nc.vector.memset(rows[:], 0.0)
        nc.scalar.dma_start(out=rows[0:4, :], in_=b.rearrange("(m p) -> m p", p=P))
        nc.scalar.dma_start(out=rows[4:12, :], in_=vb.rearrange("(m p) -> m p", p=P))
        nc.scalar.dma_start(out=rows[12:16, :], in_=k.rearrange("(m p) -> m p", p=P))
        nc.scalar.dma_start(out=tok["d"][:], in_=d.rearrange("(g p t) -> p g t", g=G, p=P))
        nc.scalar.dma_start(out=tok["c"][:], in_=c.rearrange("(g p t) -> p g t", g=G, p=P))
        ident = sb([P, P], F32, "ident")
        make_identity(nc, ident[:])

        def vec12(tag):
            return sb([P, G * J], F32, tag)

        sig, d4, c4, rsig, crs, sq, rt, r12 = [vec12(n) for n in ("sig", "d4", "c4", "rsig", "crs", "sq", "rt", "r12")]
        cols, g1 = sb([P, 16], F32, "cols"), sb([P, M], F32, "g1")
        rows32 = sb([P, P], F32, "rows32")
        dummy = sb([P, 1], F32, "dummy")
        asc = sb([P, T], F32, "asc")
        w_raw = sb([P, J, C], BF16, "w_raw")
        w_c, w_s = sb([P, C], U32, "w_c"), sb([P, C], U8, "w_s")
        v_c, v_s = sb([P, 2, 2 * C], U32, "v_c"), sb([P, 2, 2 * C], U8, "v_s")
        x_c, x_s = sb([P, G, KP], U32, "x_c"), sb([P, G, KP], U8, "x_s")
        e_c, e_s = sb([P, G, 2, KP], U32, "e_c"), sb([P, G, 2, KP], U8, "e_s")
        a_c, a_s = sb([P, G, G, KP], U32, "a_c"), sb([P, G, G, KP], U8, "a_s")
        y_c, y_s = sb([P, G, C], U32, "y_c"), sb([P, G, C], U8, "y_s")

        def flat(nm):
            return tok[nm][:].rearrange("p g t -> p (g t)")

        def copy_on(engine, out, in_):
            if engine == "S":
                nc.scalar.copy(out=out, in_=in_)
            else:
                nc.vector.tensor_copy(out=out, in_=in_)

        def quantize(grouped, codes, scales):
            nc.vector.quantize_mx(out=codes.bitcast(F8X4), scales=scales, in_=grouped.rearrange("p n j -> p (n j)"))

        def mm(bank, pairs):
            for i, (l, ls, r, rs) in enumerate(pairs):
                nc.tensor.matmul_mx(
                    out=bank, lhsT=l.bitcast(F8X4), lhsT_scale=ls, rhs=r.bitcast(F8X4), rhs_scale=rs,
                    start=(i == 0), stop=(i == len(pairs) - 1),
                )

        units = [(g, m) for hf in range(2) for g in range(G) for m in (2 * hf, 2 * hf + 1)]

        def f_d(kind, i=0, h=0):
            if kind == "x":
                st["x", i] = sb([P, J, C], BF16, "x_raw", 2)
                nc.sync.dma_start(out=st["x", i][:], in_=x_v[i])
            elif kind == "w":
                nc.sync.dma_start(out=w_raw[:], in_=w.rearrange("(p j) n -> p j n", j=J))
            elif kind == "e":
                if ("e", i) not in st:
                    st["e", i] = sb([P, J, E], BF16, "e_raw", 2)
                nc.sync.dma_start(out=st["e", i][:, 2 * h : 2 * h + 2, :], in_=e_v[i][:, 2 * h : 2 * h + 2, :])
            elif kind == "v":
                st["v", i] = sb([P, J, 2 * C], BF16, "k8", 3)
                nc.sync.dma_start(out=st["v", i][:], in_=v_v[i])
            elif kind == "a":
                st["a", i, h] = sb([P, 2, T], U8, "a_raw", 4)
                nc.sync.dma_start(out=st["a", i, h][:], in_=a_v[i][:, 2 * h : 2 * h + 2, :])
            else:
                nc.sync.dma_start(out=asc[:], in_=a_scale.rearrange("o k -> (o k)").partition_broadcast(P))

        def f_sq():
            nc.vector.tensor_copy(out=sig[:], in_=flat("sigma"))
            nc.vector.tensor_mul(out=sq[:], in0=sig[:], in1=sig[:])
            nc.vector.reciprocal(out=rsig[:], in_=sig[:])

        def f_sqrt():
            nc.scalar.activation(out=rt[:], in_=sq[:], func=ACT.Sqrt, bias=1.0)

        def f_rec():
            nc.vector.reciprocal(out=r12[:], in_=rt[:])

        def f_silud():
            nc.scalar.activation(out=dummy[:], in_=rt[:, 0:1], func=ACT.Silu)

        def f_cols1():
            nc.vector.tensor_copy(out=rows32[:], in_=rows[:])
            nc.vector.tensor_copy(out=d4[:], in_=flat("d"))
            nc.vector.tensor_copy(out=c4[:], in_=flat("c"))

        def f_colsT():
            st["cps"] = ps("tb")
            nc.tensor.transpose(st["cps"][:, 0:P], rows32[:], ident[:])

        def f_cols2():
            nc.vector.tensor_copy(out=cols[:], in_=st["cps"][:, 0:16])
            nc.vector.tensor_mul(out=crs[:], in0=c4[:], in1=rsig[:])
            nc.vector.tensor_scalar_add(out=g1[:], in0=cols[:, 4:8], scalar1=1.0)

        def f_sp(bk):
            st["sp", bk] = ps("tb")
            for q in range(J):
                col = bk * J + q
                nc.tensor.transpose(
                    st["sp", bk][:, q * P : (q + 1) * P], asv[:, col : col + 1].to_broadcast([P, P]), ident[:]
                )

        def f_spc(bk):
            nc.scalar.copy(
                out=asc[:, bk * KP : (bk + 1) * KP].rearrange("m (p q) -> m p q", q=J),
                in_=st["sp", bk][:].rearrange("m (q p) -> m p q", q=J),
            )

        def f_wcp(hf):
            n = hf * HC
            st["wg", hf] = sb([P, HC, J], BF16, "wg", 3)
            copy_on("V", st["wg", hf][:], w_raw[:, :, n : n + HC].rearrange("p j n -> p n j"))

        def f_wq(hf):
            n = hf * HC
            quantize(st["wg", hf][:], w_c[:, n : n + HC], w_s[:, n : n + HC])

        def f_vcp(hf, e, i):
            n = hf * HC + i * C
            st["vg", hf, e, i] = sb([P, HC, J], BF16, "wg", 3)
            copy_on("S" if (hf, e, i) in VS else "V", st["vg", hf, e, i][:], st["v", e][:, :, n : n + HC].rearrange("p j n -> p n j"))

        def f_vq(hf, e, i):
            n = hf * HC + i * C
            quantize(st["vg", hf, e, i][:], v_c[:, e, n : n + HC], v_s[:, e, n : n + HC])

        def f_turn(kind, g, q, h):
            if kind == "a":
                src = [st["pr", g, 2 * h + i][:] for i in range(2)]
            else:
                src = [st[kind, g][:, 2 * h + i, :] for i in range(2)]
            bank = ps("tb")
            st["tb", kind, g, q, h] = bank
            bv = bank[:].rearrange("p (i u r) -> p i u r", i=2, u=2)
            for i in range(2):
                words = src[i].bitcast(F32)
                for u in range(2):
                    nc.tensor.transpose(bv[:, i, u, :], words[:, q * 256 + u : (q + 1) * 256 : 2], ident[:])

        def f_cp(kind, g, q, h):
            if h == FIRST[kind, g, q]:
                st["gr", kind, g, q] = sb([P, KP, J], BF16, "ag" if kind == "a" else "xg", 5 if kind == "a" else 3)
            dst = st["gr", kind, g, q][:, 2 * h * P : 2 * (h + 1) * P, :].rearrange("p n j -> p (n j)").bitcast(F32)
            bv = st["tb", kind, g, q, h][:].rearrange("p (i u r) -> p i r u", i=2, u=2)
            nc.scalar.copy(out=dst.rearrange("p (i r u) -> p i r u", i=2, u=2), in_=bv)

        def f_xq(g):
            quantize(st["gr", "x", g, 0][:], x_c[:, g, :], x_s[:, g, :])

        def f_eq(g, e):
            quantize(st["gr", "e", g, e][:], e_c[:, g, e, :], e_s[:, g, e, :])

        def f_aq(g, q):
            quantize(st["gr", "a", g, q][:], a_c[:, g, q, :], a_s[:, g, q, :])

        def f_prod(g, t):
            st["pr", g, t] = sb([P, T], BF16, "prod", 6)
            nc.vector.tensor_tensor(out=st["pr", g, t][:], in0=st["a", g, t // 2][:, t % 2, :].bitcast(F8), in1=asc[:], op=MULT)

        def f_hmx(g, hf):
            cs = slice(hf * HC, (hf + 1) * HC)
            for tp in range(2):
                bank = ps("acc")
                st["p", g, hf, tp] = bank
                for i in range(2):
                    ts_ = slice((2 * tp + i) * P, (2 * tp + i + 1) * P)
                    mm(bank[:, i * HC : (i + 1) * HC], [(x_c[:, g, ts_], x_s[:, g, ts_], w_c[:, cs], w_s[:, cs])])

        def f_hr(g, hf, tp):
            if ("hr", g, hf) not in st:
                st["hr", g, hf] = sb([P, J, HC], F32, "hr", 2)
            for i in range(2):
                t = 2 * tp + i
                nc.scalar.activation(
                    out=st["hr", g, hf][:, t, :], in_=st["p", g, hf, tp][:, i * HC : (i + 1) * HC],
                    func=ACT.Copy, scale=r12[:, g * J + t : g * J + t + 1],
                )

        def v_mx(nm, n, c0):
            g, m = units[n]
            s_ = slice(c0 + m * P, c0 + (m + 1) * P)
            st[nm, n] = ps("acc")
            mm(st[nm, n][:], [(v_c[:, e, s_], v_s[:, e, s_], e_c[:, g, e, :], e_s[:, g, e, :]) for e in range(2)])

        def f_gmx(n):
            v_mx("g", n, 0)

        def f_bmx(n):
            v_mx("b", n, C)

        def f_t3(n):
            g, m = units[n]
            i = m % 2
            st["ht", n] = ps("tb")
            for t in range(J):
                nc.tensor.transpose(st["ht", n][:, t * P : (t + 1) * P], st["hr", g, m // 2][:, t, i * P : (i + 1) * P], ident[:])

        def f_h(n):
            m = units[n][1]
            st["h", n] = sb([P, KP], F32, "h", 2)
            nc.scalar.activation(out=st["h", n][:], in_=st["ht", n][:], func=ACT.Identity, bias=cols[:, m : m + 1])

        def f_kh(n):
            g, m = units[n]
            if ("kh", g, m // 2) not in st:
                st["kh", g, m // 2] = sb([P, 2, KP], F32, "kh", 2)
            nc.gpsimd.tensor_scalar(
                out=st["kh", g, m // 2][:, m % 2, :], in0=st["h", n][:],
                scalar1=cols[:, 12 + m : 13 + m], scalar2=0.0, op0=MULT, op1=ADD,
            )

        def f_z0(n):
            m = units[n][1]
            st["z0", n] = sb([P, KP], F32, "z0", 2)
            nc.vector.scalar_tensor_tensor(
                out=st["z0", n][:], in0=st["g", n][:], scalar=g1[:, m : m + 1], in1=st["h", n][:], op0=ADD, op1=MULT
            )

        def f_bt(n):
            m = units[n][1]
            st["bt", n] = sb([P, KP], F32, "bt", 2)
            if n in ZV:
                nc.vector.scalar_tensor_tensor(
                    out=st["bt", n][:], in0=st["b", n][:], scalar=cols[:, 8 + m : 9 + m], in1=st["z0", n][:], op0=ADD, op1=ADD
                )
            else:
                nc.scalar.activation(out=st["bt", n][:], in_=st["b", n][:], func=ACT.Identity, bias=cols[:, 8 + m : 9 + m])

        def f_t1(n):
            st["zt", n] = ps("tb")
            parts = ("bt",) if n in ZV else ("z0", "bt")
            for t in range(J):
                ts_ = slice(t * P, (t + 1) * P)
                for part in parts:
                    nc.tensor.matmul(
                        st["zt", n][:, ts_], lhsT=st[part, n][:, ts_], rhs=ident[:], is_transpose=True,
                        start=(part == parts[0]), stop=(part == "bt"),
                    )

        def f_silu(n):
            st["s", n] = sb([P, KP], F32, "s", 2)
            nc.scalar.activation(
                out=st["s", n][:].rearrange("p (c t) -> p c t", t=J), in_=st["zt", n][:].rearrange("p (t c) -> p c t", t=J), func=ACT.Silu
            )

        def f_y(n):
            g, m = units[n]
            if ("yg", g, m // 2) not in st:
                st["yg", g, m // 2] = sb([P, HC, J], BF16, "yg", 2)
            i = m % 2
            nc.vector.tensor_tensor(
                out=st["yg", g, m // 2][:, i * P : (i + 1) * P, :],
                in0=st["s", n][:].rearrange("p (c t) -> p c t", t=J),
                in1=d4[:, g * J : (g + 1) * J].unsqueeze(1).to_broadcast([P, P, J]),
                op=MULT,
            )

        def f_yq(g, hf):
            cs = slice(hf * HC, (hf + 1) * HC)
            quantize(st["yg", g, hf][:], y_c[:, g, cs], y_s[:, g, cs])

        def f_t2(g, hf, tp):
            kh = st["kh", g, hf]
            bank = ps("tb")
            st["kt", g, hf, tp] = bank
            for i in range(2):
                for m in range(2):
                    t = 2 * tp + i
                    nc.tensor.transpose(bank[:, (2 * i + m) * P : (2 * i + m + 1) * P], kh[:, m, t * P : (t + 1) * P], ident[:])

        def f_u(g, hf, tp):
            if ("u", g) not in st:
                st["u", g] = sb([P, J, C], F32, "k8", 3)
            for i in range(2):
                t = 2 * tp + i
                col = g * J + t
                nc.scalar.activation(
                    out=st["u", g][:, t, hf * HC : (hf + 1) * HC], in_=st["kt", g, hf, tp][:, i * HC : (i + 1) * HC],
                    func=ACT.Identity, scale=rsig[:, col : col + 1], bias=crs[:, col : col + 1],
                )

        def f_omx(g, hf, tp):
            bank = ps("acc" if hf and tp else "tb")
            st["o", g, hf, tp] = bank
            cs = slice(hf * HC, (hf + 1) * HC)
            for i in range(2):
                ts_ = slice((2 * tp + i) * P, (2 * tp + i + 1) * P)
                mm(bank[:, i * HC : (i + 1) * HC], [(a_c[:, g, q, ts_], a_s[:, g, q, ts_], y_c[:, q, cs], y_s[:, q, cs]) for q in range(G)])

        def f_ofin(g, hf, tp):
            cs = slice(hf * HC, (hf + 1) * HC)
            ut = st["u", g]
            for i in range(2):
                t = 2 * tp + i
                col = g * J + t
                nc.vector.scalar_tensor_tensor(
                    out=ut[:, t, cs], in0=st["o", g, hf, tp][:, i * HC : (i + 1) * HC], scalar=rsig[:, col : col + 1],
                    in1=ut[:, t, cs], op0=MULT, op1=ADD,
                )
            nc.sync.dma_start(out=o_v[g][:, 2 * tp : 2 * tp + 2, cs], in_=ut[:, 2 * tp : 2 * tp + 2, cs])

        steps = {
            "d": f_d, "sq": f_sq, "sqrt": f_sqrt, "rec": f_rec, "silud": f_silud, "cols1": f_cols1, "colsT": f_colsT,
            "cols2": f_cols2, "sp": f_sp, "spc": f_spc, "wcp": f_wcp, "wq": f_wq, "vcp": f_vcp, "vq": f_vq, "turn": f_turn,
            "cp": f_cp, "xq": f_xq, "eq": f_eq, "aq": f_aq, "prod": f_prod, "hmx": f_hmx, "hr": f_hr, "gmx": f_gmx,
            "bmx": f_bmx, "t3": f_t3, "h": f_h, "kh": f_kh, "z0": f_z0, "bt": f_bt, "t1": f_t1, "silu": f_silu, "y": f_y,
            "yq": f_yq, "t2": f_t2, "u": f_u, "omx": f_omx, "ofin": f_ofin,
        }
        FIRST = {}
        for stp in ORDER:
            if stp[0] == "cp":
                FIRST.setdefault(stp[1:4], stp[4])
        for stp in ORDER:
            steps[stp[0]](*stp[1:])
